import numpy as np
import ml_dtypes


def mxq(x, axis, fmt="e4m3"):
    dtype, down = {"e4m3": (ml_dtypes.float8_e4m3fn, 7), "e5m2": (ml_dtypes.float8_e5m2, 14)}[fmt]
    v = np.moveaxis(np.asarray(x, np.float32).astype(ml_dtypes.bfloat16).astype(np.float64), axis, -1)
    blocks = v.reshape(v.shape[:-1] + (-1, 32))
    amax = np.abs(blocks).max(-1, keepdims=True)
    byte = np.maximum(np.where(amax > 0, np.frexp(amax)[1] - 1 + 127, 0) - down, 1)
    scale = np.exp2(byte - 127.0)
    codes = (blocks / scale).astype(np.float32).astype(dtype).astype(np.float64)
    return np.moveaxis((codes * scale).reshape(v.shape), -1, axis)


WIDE = False


def mx_kscale(k):
    if not WIDE:
        return np.ones(k)
    levels = np.array([10, -10, 5, -5, 0])
    if k % 512:
        return np.exp2(np.random.permutation(np.resize(levels, k // 32))).repeat(32)
    a = np.empty((k // 512, 16))
    for p in range(k // 512):
        a[p, :8] = np.random.permutation(np.resize(levels, 8))
        for g in range(8):
            far = levels[np.abs(levels - a[p, g]) >= 10]
            a[p, g + 8] = far[np.random.randint(len(far))]
    return np.exp2(a.ravel()).repeat(32)


def f64(x):
    return np.asarray(x).astype(np.float64)


def striped(idx):
    return np.tile(idx.reshape(-1, 16).T, (8, 1)).astype(np.uint16)


def unstriped(offs):
    return offs[:16].T.reshape(-1).astype(np.int64)


def gelu(v):
    return 0.5 * v * (1.0 + np.tanh(np.sqrt(2.0 / np.pi) * (v + 0.044715 * v**3)))


K, T, S, H, N = 512, 2048, 768, 512, 128


def setup_inputs():
    n = np.random.standard_normal
    s = mx_kscale(K)[:, None]
    u = mx_kscale(H)
    return {
        "xT": (n((K, T)) * s).astype(np.float32),
        "w1": (n((K, H)) / np.sqrt(K) / s * u).astype(np.float32),
        "w2": (n((H, N)) / np.sqrt(H) / u[:, None]).astype(np.float32),
        "offs": striped(np.random.permutation(T)[:S]),
    }


def reference(xT, w1, w2, offs):
    idx = unstriped(offs)
    xq = mxq(f64(xT)[:, idx], 0, "e4m3")
    h = gelu(mxq(f64(w1), 0, "e4m3").T @ xq)
    y = mxq(f64(w2), 0, "e4m3").T @ mxq(h, 0, "e4m3")
    return y

@@ -1,0 +1,216 @@
+from contextlib import ExitStack
+
+import concourse.mybir as mybir
+from concourse.masks import make_identity
+
+K, T, S, H, N = 512, 2048, 768, 512, 128
+FLOPS = 2 * S * H * (K + N)
+
+F32 = mybir.dt.float32
+BF16 = mybir.dt.bfloat16
+U32 = mybir.dt.uint32
+U16 = mybir.dt.uint16
+U8 = mybir.dt.uint8
+FP8X4 = mybir.dt.float8_e4m3fn_x4
+GELU = mybir.ActivationFunctionType.Gelu_apprx_tanh
+
+P = 128
+PACK = 4
+SLICE = 256
+GROUP = 128
+ALIGN = 64
+W1_SCALAR = 48
+
+
+def quantize(nc, codes, scales, values):
+    nc.vector.quantize_mx(out=codes.bitcast(FP8X4), scales=scales, in_=values)
+
+
+def tile_picked_pick_mlp_gelu_sub_e_kernel(tc, xT, w1, w2, offs, out):
+    nc = tc.nc
+    slices = S // SLICE
+    per_slice = SLICE // GROUP
+    groups = S // GROUP
+
+    with ExitStack() as ctx:
+        keep = ctx.enter_context(tc.tile_pool(name="keep", bufs=1))
+        psum = ctx.enter_context(tc.psum_pool(name="psum", bufs=1))
+
+        offsets = keep.tile([P, S // 16], U16, name="offsets")
+        nc.sync.dma_start(offsets[:], offs)
+
+        w1_raw = keep.tile([P, PACK, H], F32, name="w1_raw")
+        nc.sync.dma_start(out=w1_raw[:], in_=w1.rearrange("(p j) h -> p j h", j=PACK))
+        planes = []
+        x_rows = xT.rearrange("(p j) t -> p j t", j=PACK)
+        for j in range(PACK):
+            plane = keep.tile([P, T], F32, name=f"plane{j}")
+            nc.sync.dma_start(out=plane[:], in_=x_rows[:, j, :])
+            planes.append(plane)
+        w2_raw = keep.tile([P, PACK, N], F32, name="w2_raw")
+        nc.sync.dma_start(out=w2_raw[:], in_=w2.rearrange("(p j) n -> p j n", j=PACK))
+
+        probe = keep.tile([P, 1], F32, name="probe")
+        nc.vector.memset(probe[:], 0.0)
+        probe_out = keep.tile([P, 1], F32, name="probe_out")
+        nc.scalar.activation(probe_out[:], probe[:], GELU)
+
+        early = PACK // 2
+        identity = keep.tile([P, P], F32, name="identity")
+        make_identity(nc, identity[:])
+        warm = psum.tile([P, PACK, P], F32, name="warm", tag="y_bank0")
+        picked = keep.tile([P, PACK, S], F32, name="picked")
+        nc.gpsimd.memset(picked[:, early:, :], 0.0)
+
+        w1_grouped = keep.tile([P, H * PACK], BF16, name="w1_grouped", align_bytes=ALIGN)
+        w1_to = w1_grouped[:].rearrange("p (t m j) -> p m j t", t=PACK, j=PACK)
+        w1_from = w1_raw[:].rearrange("p j (m t) -> p m j t", t=PACK)
+        nc.scalar.copy(w1_to[:, :W1_SCALAR], w1_from[:, :W1_SCALAR])
+        nc.vector.tensor_copy(w1_to[:, W1_SCALAR:], w1_from[:, W1_SCALAR:])
+        w1_codes = keep.tile([P, H], U32, name="w1_codes", align_bytes=ALIGN)
+        w1_scales = keep.tile([P, H], U8, name="w1_scales", align_bytes=ALIGN)
+        quantize(nc, w1_codes[:], w1_scales[:], w1_grouped[:])
+
+        x_grouped = []
+        for s in range(slices):
+            tile = keep.tile([P, SLICE, PACK], BF16, name=f"x_grouped{s}", align_bytes=ALIGN)
+            x_grouped.append(tile)
+
+        def entries(s):
+            return offsets[:, s * (SLICE // 16) : (s + 1) * (SLICE // 16)]
+
+        def part(s):
+            return slice(s * SLICE, (s + 1) * SLICE)
+
+        def gather_plain(j, s):
+            nc.vector.tensor_copy(picked[:, j, part(s)], planes[j][:].indirect(entries(s)))
+
+        def gather_stepped(j, s):
+            nc.vector.tensor_copy(x_grouped[s][:, :, j], planes[j][:].indirect(entries(s)))
+
+        def interleave(s):
+            nc.scalar.copy(
+                x_grouped[s][:].rearrange("p (c i) t -> p c t i", i=4),
+                picked[:, :, part(s)].rearrange("p t (c i) -> p c t i", i=4),
+            )
+
+        nc.vector.tensor_copy(picked[:, 0, :], planes[0][:].indirect(offsets[:]))
+        for s in range(slices):
+            gather_plain(1, s)
+        interleave(0)
+        for i in range(18):
+            block = slice((i % 16) * P, (i % 16 + 1) * P)
+            nc.tensor.transpose(warm[:, i % PACK, :], planes[2][:, block], identity[:])
+        gather_plain(2, 1)
+        interleave(1)
+        gather_plain(2, 2)
+        gather_stepped(2, 0)
+        interleave(2)
+
+        w2_grouped = keep.tile([P, N, PACK], BF16, name="w2_grouped", align_bytes=ALIGN)
+
+        x_codes = keep.tile([P, S], U32, name="x_codes", align_bytes=ALIGN)
+        x_scales = keep.tile([P, S], U8, name="x_scales", align_bytes=ALIGN)
+        h_codes = keep.tile([P, S], U32, name="h_codes", align_bytes=ALIGN)
+        h_scales = keep.tile([P, S], U8, name="h_scales", align_bytes=ALIGN)
+        w2_codes = keep.tile([P, N], U32, name="w2_codes", align_bytes=ALIGN)
+        w2_scales = keep.tile([P, N], U8, name="w2_scales", align_bytes=ALIGN)
+        result = keep.tile([P, S], F32, name="result")
+        h_banks = []
+        for g in range(groups):
+            bank = psum.tile([P, PACK, GROUP], F32, name=f"h_bank{g}")
+            h_banks.append(bank)
+        h_grouped = keep.tile([P, S, PACK], BF16, name="h_grouped", align_bytes=ALIGN)
+
+        def quantize_x(start, width):
+            cols = slice(start, start + width)
+            s = start // SLICE
+            own = slice(start % SLICE, start % SLICE + width)
+            quantize(nc, x_codes[:, cols], x_scales[:, cols], x_grouped[s][:, own, :].rearrange("p n t -> p (n t)"))
+
+        def first_layer(g):
+            cols = slice(g * GROUP, (g + 1) * GROUP)
+            for t in range(PACK):
+                w_cols = slice(t * P, (t + 1) * P)
+                nc.tensor.matmul_mx(
+                    out=h_banks[g][:, t, :],
+                    lhsT=w1_codes[:, w_cols].bitcast(FP8X4),
+                    lhsT_scale=w1_scales[:, w_cols],
+                    rhs=x_codes[:, cols].bitcast(FP8X4),
+                    rhs_scale=x_scales[:, cols],
+                    start=True,
+                    stop=True,
+                )
+
+        def gelu(start, width):
+            cols = slice(start, start + width)
+            own = slice(start % GROUP, start % GROUP + width)
+            bank = h_banks[start // GROUP]
+            nc.scalar.activation(h_grouped[:, cols, :], bank[:, :, own].rearrange("p t n -> p n t"), GELU)
+
+        def quantize_h(start, width):
+            cols = slice(start, start + width)
+            quantize(nc, h_codes[:, cols], h_scales[:, cols], h_grouped[:, cols, :].rearrange("p n t -> p (n t)"))
+
+        def second_layer(y, start, width):
+            cols = slice(start, start + width)
+            nc.tensor.matmul_mx(
+                out=y,
+                lhsT=w2_codes[:].bitcast(FP8X4),
+                lhsT_scale=w2_scales[:],
+                rhs=h_codes[:, cols].bitcast(FP8X4),
+                rhs_scale=h_scales[:, cols],
+                start=True,
+                stop=True,
+            )
+
+        def hold(s):
+            nc.vector.tensor_copy(x_grouped[s][:, 0, PACK - 1 :], x_grouped[s + 1][:, 0, PACK - 1 :])
+
+        gather_stepped(3, 0)
+        quantize_x(0, GROUP)
+        hold(0)
+        quantize_x(GROUP, GROUP)
+        first_layer(0)
+        nc.scalar.copy(
+            w2_grouped[:].rearrange("p (c i) t -> p c t i", i=4), w2_raw[:].rearrange("p t (c i) -> p c t i", i=4)
+        )
+        gelu(0, GROUP)
+        first_layer(1)
+        gelu(GROUP, GROUP)
+        gather_stepped(3, 1)
+        quantize_x(SLICE, GROUP)
+        hold(1)
+        quantize_x(SLICE + GROUP, GROUP)
+        first_layer(2)
+        gelu(2 * GROUP, GROUP)
+        first_layer(3)
+        gelu(3 * GROUP, GROUP)
+        gather_stepped(3, 2)
+        quantize_x(2 * SLICE, SLICE)
+        quantize(nc, w2_codes[:], w2_scales[:], w2_grouped[:].rearrange("p n t -> p (n t)"))
+        first_layer(4)
+        gelu(4 * GROUP, GROUP)
+        first_layer(5)
+        gelu(5 * GROUP, GROUP // 2)
+        gelu(5 * GROUP + GROUP // 2, GROUP // 2)
+        y_banks = []
+        for s in range(2):
+            bank = psum.tile([P, SLICE], F32, name=f"y_bank{s}")
+            y_banks.append(bank)
+        y_fifth = psum.tile([P, GROUP], F32, name="y_fifth", tag="h_bank0")
+        y_sixth = psum.tile([P, GROUP], F32, name="y_sixth", tag="h_bank1")
+        for s in range(2):
+            quantize_h(s * SLICE, SLICE)
+            second_layer(y_banks[s][:], s * SLICE, SLICE)
+            nc.vector.tensor_copy(result[:, part(s)], y_banks[s][:])
+        nc.sync.dma_start(out=out[:, : 2 * SLICE], in_=result[:, : 2 * SLICE])
+        quantize_h(4 * GROUP, GROUP)
+        second_layer(y_fifth[:], 4 * GROUP, GROUP)
+        nc.scalar.copy(result[:, 4 * GROUP : 5 * GROUP], y_fifth[:])
+        nc.sync.dma_start(out=out[:, 4 * GROUP : 5 * GROUP], in_=result[:, 4 * GROUP : 5 * GROUP])
+        for start in (0, GROUP // 2):
+            quantize_h(5 * GROUP + start, GROUP // 2)
+            second_layer(y_sixth[:, start : start + GROUP // 2], 5 * GROUP + start, GROUP // 2)
+        nc.vector.tensor_copy(result[:, 5 * GROUP :], y_sixth[:])
+        nc.sync.dma_start(out=out[:, 5 * GROUP :], in_=result[:, 5 * GROUP :])

@@ -1,7 +1,6 @@
 from contextlib import ExitStack
 
 import concourse.mybir as mybir
-from concourse.masks import make_identity
 
 K, T, S, H, N = 512, 2048, 768, 512, 128
 FLOPS = 2 * S * H * (K + N)
@@ -19,6 +18,7 @@ PACK = 4
 SLICE = 256
 GROUP = 128
 ALIGN = 64
+HALF = P // 2
 W1_SCALAR = 48
 
 
@@ -29,7 +29,6 @@ def quantize(nc, codes, scales, values):
 def tile_picked_pick_mlp_gelu_sub_e_kernel(tc, xT, w1, w2, offs, out):
     nc = tc.nc
     slices = S // SLICE
-    per_slice = SLICE // GROUP
     groups = S // GROUP
 
     with ExitStack() as ctx:
@@ -37,16 +36,20 @@ def tile_picked_pick_mlp_gelu_sub_e_kernel(tc, xT, w1, w2, offs, out):
         psum = ctx.enter_context(tc.psum_pool(name="psum", bufs=1))
 
         offsets = keep.tile([P, S // 16], U16, name="offsets")
-        nc.sync.dma_start(offsets[:], offs)
-
-        w1_raw = keep.tile([P, PACK, H], F32, name="w1_raw")
-        nc.sync.dma_start(out=w1_raw[:], in_=w1.rearrange("(p j) h -> p j h", j=PACK))
         planes = []
         x_rows = xT.rearrange("(p j) t -> p j t", j=PACK)
         for j in range(PACK):
             plane = keep.tile([P, T], F32, name=f"plane{j}")
             nc.sync.dma_start(out=plane[:], in_=x_rows[:, j, :])
             planes.append(plane)
+            if j == 0:
+                nc.sync.dma_start(offsets[:], offs)
+        w1_rows = w1.rearrange("(p j) h -> p j h", j=PACK)
+        w1_raw = []
+        for half in range(2):
+            raw = keep.tile([P, PACK, H // 2], F32, name=f"w1_raw{half}")
+            nc.sync.dma_start(out=raw[:], in_=w1_rows[:, :, half * (H // 2) : (half + 1) * (H // 2)])
+            w1_raw.append(raw)
         w2_raw = keep.tile([P, PACK, N], F32, name="w2_raw")
         nc.sync.dma_start(out=w2_raw[:], in_=w2.rearrange("(p j) n -> p j n", j=PACK))
 
@@ -56,21 +59,7 @@ def tile_picked_pick_mlp_gelu_sub_e_kernel(tc, xT, w1, w2, offs, out):
         nc.scalar.activation(probe_out[:], probe[:], GELU)
 
         early = PACK // 2
-        identity = keep.tile([P, P], F32, name="identity")
-        make_identity(nc, identity[:])
-        warm = psum.tile([P, PACK, P], F32, name="warm", tag="y_bank0")
-        picked = keep.tile([P, PACK, S], F32, name="picked")
-        nc.gpsimd.memset(picked[:, early:, :], 0.0)
-
-        w1_grouped = keep.tile([P, H * PACK], BF16, name="w1_grouped", align_bytes=ALIGN)
-        w1_to = w1_grouped[:].rearrange("p (t m j) -> p m j t", t=PACK, j=PACK)
-        w1_from = w1_raw[:].rearrange("p j (m t) -> p m j t", t=PACK)
-        nc.scalar.copy(w1_to[:, :W1_SCALAR], w1_from[:, :W1_SCALAR])
-        nc.vector.tensor_copy(w1_to[:, W1_SCALAR:], w1_from[:, W1_SCALAR:])
-        w1_codes = keep.tile([P, H], U32, name="w1_codes", align_bytes=ALIGN)
-        w1_scales = keep.tile([P, H], U8, name="w1_scales", align_bytes=ALIGN)
-        quantize(nc, w1_codes[:], w1_scales[:], w1_grouped[:])
-
+        picked = keep.tile([P, early, S], F32, name="picked")
         x_grouped = []
         for s in range(slices):
             tile = keep.tile([P, SLICE, PACK], BF16, name=f"x_grouped{s}", align_bytes=ALIGN)
@@ -82,51 +71,68 @@ def tile_picked_pick_mlp_gelu_sub_e_kernel(tc, xT, w1, w2, offs, out):
         def part(s):
             return slice(s * SLICE, (s + 1) * SLICE)
 
-        def gather_plain(j, s):
-            nc.vector.tensor_copy(picked[:, j, part(s)], planes[j][:].indirect(entries(s)))
-
         def gather_stepped(j, s):
             nc.vector.tensor_copy(x_grouped[s][:, :, j], planes[j][:].indirect(entries(s)))
 
-        def interleave(s):
-            nc.scalar.copy(
-                x_grouped[s][:].rearrange("p (c i) t -> p c t i", i=4),
-                picked[:, :, part(s)].rearrange("p t (c i) -> p c t i", i=4),
-            )
-
         nc.vector.tensor_copy(picked[:, 0, :], planes[0][:].indirect(offsets[:]))
         for s in range(slices):
-            gather_plain(1, s)
-        interleave(0)
-        for i in range(18):
-            block = slice((i % 16) * P, (i % 16 + 1) * P)
-            nc.tensor.transpose(warm[:, i % PACK, :], planes[2][:, block], identity[:])
-        gather_plain(2, 1)
-        interleave(1)
-        gather_plain(2, 2)
-        gather_stepped(2, 0)
-        interleave(2)
+            nc.vector.tensor_copy(picked[:, 1, part(s)], planes[1][:].indirect(entries(s)))
+            nc.scalar.copy(
+                x_grouped[s][:, :, :early].rearrange("p (c i) t -> p c t i", i=4),
+                picked[:, :, part(s)].rearrange("p t (c i) -> p c t i", i=4),
+            )
+        for j in range(early, PACK):
+            for s in range(slices):
+                gather_stepped(j, s)
+
+        x_codes_first = keep.tile([P, SLICE], U32, name="x_codes_first", align_bytes=ALIGN)
+        x_scales = keep.tile([P, S], U8, name="x_scales", align_bytes=ALIGN)
+
+        def quantize_x(codes, s):
+            quantize(nc, codes, x_scales[:, part(s)], x_grouped[s][:].rearrange("p n t -> p (n t)"))
+
+        quantize_x(x_codes_first[:], 0)
+
+        w1_codes = keep.tile([P, H], U32, name="w1_codes", align_bytes=ALIGN)
+        w1_scales = keep.tile([P, H], U8, name="w1_scales", align_bytes=ALIGN)
+        for half in range(2):
+            grouped = keep.tile([P, PACK, HALF * PACK], BF16, name=f"w1_grouped{half}", align_bytes=ALIGN)
+            w1_to = grouped[:].rearrange("p t (m j) -> p m j t", j=PACK)
+            w1_from = w1_raw[half][:].rearrange("p j (m t) -> p m j t", t=PACK)
+            if half == 0:
+                nc.scalar.copy(w1_to, w1_from)
+            else:
+                nc.scalar.copy(w1_to[:, :W1_SCALAR], w1_from[:, :W1_SCALAR])
+                nc.vector.tensor_copy(w1_to[:, W1_SCALAR:], w1_from[:, W1_SCALAR:])
+            for t in range(PACK):
+                cols = slice(t * P + half * HALF, t * P + (half + 1) * HALF)
+                quantize(nc, w1_codes[:, cols], w1_scales[:, cols], grouped[:, t, :])
+
+        x_codes_rest = keep.tile([P, S - SLICE], U32, name="x_codes_rest", tag="w1_grouped1", align_bytes=ALIGN)
+        for s in range(1, slices):
+            quantize_x(x_codes_rest[:, part(s - 1)], s)
+
+        def x_codes(g):
+            if g * GROUP < SLICE:
+                return x_codes_first[:, g * GROUP : (g + 1) * GROUP]
+            return x_codes_rest[:, g * GROUP - SLICE : (g + 1) * GROUP - SLICE]
 
         w2_grouped = keep.tile([P, N, PACK], BF16, name="w2_grouped", align_bytes=ALIGN)
-
-        x_codes = keep.tile([P, S], U32, name="x_codes", align_bytes=ALIGN)
-        x_scales = keep.tile([P, S], U8, name="x_scales", align_bytes=ALIGN)
-        h_codes = keep.tile([P, S], U32, name="h_codes", align_bytes=ALIGN)
-        h_scales = keep.tile([P, S], U8, name="h_scales", align_bytes=ALIGN)
+        nc.scalar.copy(
+            w2_grouped[:].rearrange("p (c i) t -> p c t i", i=4), w2_raw[:].rearrange("p t (c i) -> p c t i", i=4)
+        )
         w2_codes = keep.tile([P, N], U32, name="w2_codes", align_bytes=ALIGN)
         w2_scales = keep.tile([P, N], U8, name="w2_scales", align_bytes=ALIGN)
+        quantize(nc, w2_codes[:], w2_scales[:], w2_grouped[:].rearrange("p n t -> p (n t)"))
+
+        h_codes = keep.tile([P, S], U32, name="h_codes", align_bytes=ALIGN)
+        h_scales = keep.tile([P, S], U8, name="h_scales", align_bytes=ALIGN)
         result = keep.tile([P, S], F32, name="result")
         h_banks = []
         for g in range(groups):
             bank = psum.tile([P, PACK, GROUP], F32, name=f"h_bank{g}")
             h_banks.append(bank)
         h_grouped = keep.tile([P, S, PACK], BF16, name="h_grouped", align_bytes=ALIGN)
-
-        def quantize_x(start, width):
-            cols = slice(start, start + width)
-            s = start // SLICE
-            own = slice(start % SLICE, start % SLICE + width)
-            quantize(nc, x_codes[:, cols], x_scales[:, cols], x_grouped[s][:, own, :].rearrange("p n t -> p (n t)"))
 
         def first_layer(g):
             cols = slice(g * GROUP, (g + 1) * GROUP)
@@ -136,7 +142,7 @@ def tile_picked_pick_mlp_gelu_sub_e_kernel(tc, xT, w1, w2, offs, out):
                     out=h_banks[g][:, t, :],
                     lhsT=w1_codes[:, w_cols].bitcast(FP8X4),
                     lhsT_scale=w1_scales[:, w_cols],
-                    rhs=x_codes[:, cols].bitcast(FP8X4),
+                    rhs=x_codes(g).bitcast(FP8X4),
                     rhs_scale=x_scales[:, cols],
                     start=True,
                     stop=True,
@@ -164,33 +170,9 @@ def tile_picked_pick_mlp_gelu_sub_e_kernel(tc, xT, w1, w2, offs, out):
                 stop=True,
             )
 
-        def hold(s):
-            nc.vector.tensor_copy(x_grouped[s][:, 0, PACK - 1 :], x_grouped[s + 1][:, 0, PACK - 1 :])
-
-        gather_stepped(3, 0)
-        quantize_x(0, GROUP)
-        hold(0)
-        quantize_x(GROUP, GROUP)
-        first_layer(0)
-        nc.scalar.copy(
-            w2_grouped[:].rearrange("p (c i) t -> p c t i", i=4), w2_raw[:].rearrange("p t (c i) -> p c t i", i=4)
-        )
-        gelu(0, GROUP)
-        first_layer(1)
-        gelu(GROUP, GROUP)
-        gather_stepped(3, 1)
-        quantize_x(SLICE, GROUP)
-        hold(1)
-        quantize_x(SLICE + GROUP, GROUP)
-        first_layer(2)
-        gelu(2 * GROUP, GROUP)
-        first_layer(3)
-        gelu(3 * GROUP, GROUP)
-        gather_stepped(3, 2)
-        quantize_x(2 * SLICE, SLICE)
-        quantize(nc, w2_codes[:], w2_scales[:], w2_grouped[:].rearrange("p n t -> p (n t)"))
-        first_layer(4)
-        gelu(4 * GROUP, GROUP)
+        for g in range(groups - 1):
+            first_layer(g)
+            gelu(g * GROUP, GROUP)
         first_layer(5)
         gelu(5 * GROUP, GROUP // 2)
         gelu(5 * GROUP + GROUP // 2, GROUP // 2)

@@ -19,7 +19,7 @@ SLICE = 256
 GROUP = 128
 ALIGN = 64
 HALF = P // 2
-W1_SCALAR = 48
+W1_SCALAR = 24
 
 
 def quantize(nc, codes, scales, values):
@@ -33,6 +33,7 @@ def tile_picked_pick_mlp_gelu_sub_e_kernel(tc, xT, w1, w2, offs, out):
 
     with ExitStack() as ctx:
         keep = ctx.enter_context(tc.tile_pool(name="keep", bufs=1))
+        late = ctx.enter_context(tc.tile_pool(name="late", bufs=1))
         psum = ctx.enter_context(tc.psum_pool(name="psum", bufs=1))
 
         offsets = keep.tile([P, S // 16], U16, name="offsets")
@@ -81,9 +82,10 @@ def tile_picked_pick_mlp_gelu_sub_e_kernel(tc, xT, w1, w2, offs, out):
                 x_grouped[s][:, :, :early].rearrange("p (c i) t -> p c t i", i=4),
                 picked[:, :, part(s)].rearrange("p t (c i) -> p c t i", i=4),
             )
-        for j in range(early, PACK):
-            for s in range(slices):
-                gather_stepped(j, s)
+        for s in range(slices):
+            gather_stepped(2, s)
+        for s in range(slices - 1):
+            gather_stepped(3, s)
 
         x_codes_first = keep.tile([P, SLICE], U32, name="x_codes_first", align_bytes=ALIGN)
         x_scales = keep.tile([P, S], U8, name="x_scales", align_bytes=ALIGN)
@@ -96,7 +98,9 @@ def tile_picked_pick_mlp_gelu_sub_e_kernel(tc, xT, w1, w2, offs, out):
         w1_codes = keep.tile([P, H], U32, name="w1_codes", align_bytes=ALIGN)
         w1_scales = keep.tile([P, H], U8, name="w1_scales", align_bytes=ALIGN)
         for half in range(2):
-            grouped = keep.tile([P, PACK, HALF * PACK], BF16, name=f"w1_grouped{half}", align_bytes=ALIGN)
+            grouped = late.tile(
+                [P, PACK, HALF * PACK], BF16, name=f"w1_grouped{half}", align_bytes=ALIGN, offset=half * 2048
+            )
             w1_to = grouped[:].rearrange("p t (m j) -> p m j t", j=PACK)
             w1_from = w1_raw[half][:].rearrange("p j (m t) -> p m j t", t=PACK)
             if half == 0:
@@ -108,14 +112,18 @@ def tile_picked_pick_mlp_gelu_sub_e_kernel(tc, xT, w1, w2, offs, out):
                 cols = slice(t * P + half * HALF, t * P + (half + 1) * HALF)
                 quantize(nc, w1_codes[:, cols], w1_scales[:, cols], grouped[:, t, :])
 
-        x_codes_rest = keep.tile([P, S - SLICE], U32, name="x_codes_rest", tag="w1_grouped1", align_bytes=ALIGN)
-        for s in range(1, slices):
-            quantize_x(x_codes_rest[:, part(s - 1)], s)
+        x_codes_second = late.tile([P, SLICE], U32, name="x_codes_second", align_bytes=ALIGN, offset=2048)
+        quantize_x(x_codes_second[:], 1)
+        last_plane = late.tile([P, SLICE], F32, name="last_plane", align_bytes=ALIGN, offset=3072)
+        nc.vector.tensor_copy(last_plane[:], planes[3][:].indirect(entries(2)))
+        nc.vector.tensor_copy(x_grouped[2][:, :, 3], last_plane[:])
+        x_codes_third = keep.tile([P, SLICE], U32, name="x_codes_third", align_bytes=ALIGN)
+        quantize_x(x_codes_third[:], 2)
+        x_tiles = [x_codes_first, x_codes_second, x_codes_third]
 
         def x_codes(g):
-            if g * GROUP < SLICE:
-                return x_codes_first[:, g * GROUP : (g + 1) * GROUP]
-            return x_codes_rest[:, g * GROUP - SLICE : (g + 1) * GROUP - SLICE]
+            start = g * GROUP % SLICE
+            return x_tiles[g * GROUP // SLICE][:, start : start + GROUP]
 
         w2_grouped = keep.tile([P, N, PACK], BF16, name="w2_grouped", align_bytes=ALIGN)
         nc.scalar.copy(
@@ -185,12 +193,13 @@ def tile_picked_pick_mlp_gelu_sub_e_kernel(tc, xT, w1, w2, offs, out):
         for s in range(2):
             quantize_h(s * SLICE, SLICE)
             second_layer(y_banks[s][:], s * SLICE, SLICE)
-            nc.vector.tensor_copy(result[:, part(s)], y_banks[s][:])
-        nc.sync.dma_start(out=out[:, : 2 * SLICE], in_=result[:, : 2 * SLICE])
+        nc.vector.tensor_copy(result[:, part(0)], y_banks[0][:])
+        nc.sync.dma_start(out=out[:, part(0)], in_=result[:, part(0)])
+        nc.scalar.copy(result[:, part(1)], y_banks[1][:])
         quantize_h(4 * GROUP, GROUP)
         second_layer(y_fifth[:], 4 * GROUP, GROUP)
         nc.scalar.copy(result[:, 4 * GROUP : 5 * GROUP], y_fifth[:])
-        nc.sync.dma_start(out=out[:, 4 * GROUP : 5 * GROUP], in_=result[:, 4 * GROUP : 5 * GROUP])
+        nc.sync.dma_start(out=out[:, SLICE : 5 * GROUP], in_=result[:, SLICE : 5 * GROUP])
         for start in (0, GROUP // 2):
             quantize_h(5 * GROUP + start, GROUP // 2)
             second_layer(y_sixth[:, start : start + GROUP // 2], 5 * GROUP + start, GROUP // 2)

@@ -59,8 +59,7 @@ def tile_picked_pick_mlp_gelu_sub_e_kernel(tc, xT, w1, w2, offs, out):
         probe_out = keep.tile([P, 1], F32, name="probe_out")
         nc.scalar.activation(probe_out[:], probe[:], GELU)
 
-        early = PACK // 2
-        picked = keep.tile([P, early, S], F32, name="picked")
+        picked = keep.tile([P, slices * (PACK - 1), SLICE], F32, name="picked")
         x_grouped = []
         for s in range(slices):
             tile = keep.tile([P, SLICE, PACK], BF16, name=f"x_grouped{s}", align_bytes=ALIGN)
@@ -75,15 +74,23 @@ def tile_picked_pick_mlp_gelu_sub_e_kernel(tc, xT, w1, w2, offs, out):
         def gather_stepped(j, s):
             nc.vector.tensor_copy(x_grouped[s][:, :, j], planes[j][:].indirect(entries(s)))
 
-        nc.vector.tensor_copy(picked[:, 0, :], planes[0][:].indirect(offsets[:]))
-        for s in range(slices):
-            nc.vector.tensor_copy(picked[:, 1, part(s)], planes[1][:].indirect(entries(s)))
+        def gather_plain(j, s):
+            nc.vector.tensor_copy(picked[:, (PACK - 1) * s + j, :], planes[j][:].indirect(entries(s)))
+
+        def interleave(s, count):
             nc.scalar.copy(
-                x_grouped[s][:, :, :early].rearrange("p (c i) t -> p c t i", i=4),
-                picked[:, :, part(s)].rearrange("p t (c i) -> p c t i", i=4),
+                x_grouped[s][:, :, :count].rearrange("p (c i) t -> p c t i", i=4),
+                picked[:, (PACK - 1) * s : (PACK - 1) * s + count, :].rearrange("p t (c i) -> p c t i", i=4),
             )
-        for s in range(slices):
-            gather_stepped(2, s)
+
+        for j in range(2):
+            for s in range(slices):
+                gather_plain(j, s)
+        interleave(2, 2)
+        for s in range(slices - 1):
+            gather_plain(2, s)
+            interleave(s, PACK)
+        gather_stepped(2, 2)
         for s in range(slices - 1):
             gather_stepped(3, s)
 
@@ -113,9 +120,9 @@ def tile_picked_pick_mlp_gelu_sub_e_kernel(tc, xT, w1, w2, offs, out):
                 quantize(nc, w1_codes[:, cols], w1_scales[:, cols], grouped[:, t, :])
 
         x_codes_second = late.tile([P, SLICE], U32, name="x_codes_second", align_bytes=ALIGN, offset=2048)
-        quantize_x(x_codes_second[:], 1)
         last_plane = late.tile([P, SLICE], F32, name="last_plane", align_bytes=ALIGN, offset=3072)
         nc.vector.tensor_copy(last_plane[:], planes[3][:].indirect(entries(2)))
+        quantize_x(x_codes_second[:], 1)
         nc.vector.tensor_copy(x_grouped[2][:, :, 3], last_plane[:])
         x_codes_third = keep.tile([P, SLICE], U32, name="x_codes_third", align_bytes=ALIGN)
         quantize_x(x_codes_third[:], 2)

@@ -203,12 +203,12 @@ def tile_picked_pick_mlp_gelu_sub_e_kernel(tc, xT, w1, w2, offs, out):
         nc.vector.tensor_copy(result[:, part(0)], y_banks[0][:])
         nc.sync.dma_start(out=out[:, part(0)], in_=result[:, part(0)])
         nc.scalar.copy(result[:, part(1)], y_banks[1][:])
+        nc.sync.dma_start(out=out[:, part(1)], in_=result[:, part(1)])
         quantize_h(4 * GROUP, GROUP)
         second_layer(y_fifth[:], 4 * GROUP, GROUP)
         nc.scalar.copy(result[:, 4 * GROUP : 5 * GROUP], y_fifth[:])
-        nc.sync.dma_start(out=out[:, SLICE : 5 * GROUP], in_=result[:, SLICE : 5 * GROUP])
         for start in (0, GROUP // 2):
             quantize_h(5 * GROUP + start, GROUP // 2)
             second_layer(y_sixth[:, start : start + GROUP // 2], 5 * GROUP + start, GROUP // 2)
         nc.vector.tensor_copy(result[:, 5 * GROUP :], y_sixth[:])
-        nc.sync.dma_start(out=out[:, 5 * GROUP :], in_=result[:, 5 * GROUP :])
+        nc.sync.dma_start(out=out[:, part(2)], in_=result[:, part(2)])

@@ -19,7 +19,6 @@ SLICE = 256
 GROUP = 128
 ALIGN = 64
 HALF = P // 2
-W1_SCALAR = 24
 
 
 def quantize(nc, codes, scales, values):
@@ -47,9 +46,9 @@ def tile_picked_pick_mlp_gelu_sub_e_kernel(tc, xT, w1, w2, offs, out):
                 nc.sync.dma_start(offsets[:], offs)
         w1_rows = w1.rearrange("(p j) h -> p j h", j=PACK)
         w1_raw = []
-        for half in range(2):
-            raw = keep.tile([P, PACK, H // 2], F32, name=f"w1_raw{half}")
-            nc.sync.dma_start(out=raw[:], in_=w1_rows[:, :, half * (H // 2) : (half + 1) * (H // 2)])
+        for start, width in ((0, H // 2), (H // 2, H // 4), (3 * H // 4, H // 4)):
+            raw = keep.tile([P, PACK, width], F32, name=f"w1_raw{start}")
+            nc.sync.dma_start(out=raw[:], in_=w1_rows[:, :, start : start + width])
             w1_raw.append(raw)
         w2_raw = keep.tile([P, PACK, N], F32, name="w2_raw")
         nc.sync.dma_start(out=w2_raw[:], in_=w2.rearrange("(p j) n -> p j n", j=PACK))
@@ -86,11 +85,12 @@ def tile_picked_pick_mlp_gelu_sub_e_kernel(tc, xT, w1, w2, offs, out):
         for j in range(2):
             for s in range(slices):
                 gather_plain(j, s)
-        interleave(2, 2)
-        for s in range(slices - 1):
-            gather_plain(2, s)
-            interleave(s, PACK)
-        gather_stepped(2, 2)
+        for s in range(1, slices):
+            interleave(s, 2)
+        gather_plain(2, 0)
+        interleave(0, PACK)
+        for s in range(1, slices):
+            gather_stepped(2, s)
         for s in range(slices - 1):
             gather_stepped(3, s)
 
@@ -109,12 +109,12 @@ def tile_picked_pick_mlp_gelu_sub_e_kernel(tc, xT, w1, w2, offs, out):
                 [P, PACK, HALF * PACK], BF16, name=f"w1_grouped{half}", align_bytes=ALIGN, offset=half * 2048
             )
             w1_to = grouped[:].rearrange("p t (m j) -> p m j t", j=PACK)
-            w1_from = w1_raw[half][:].rearrange("p j (m t) -> p m j t", t=PACK)
             if half == 0:
-                nc.scalar.copy(w1_to, w1_from)
+                nc.scalar.copy(w1_to, w1_raw[0][:].rearrange("p j (m t) -> p m j t", t=PACK))
             else:
-                nc.scalar.copy(w1_to[:, :W1_SCALAR], w1_from[:, :W1_SCALAR])
-                nc.vector.tensor_copy(w1_to[:, W1_SCALAR:], w1_from[:, W1_SCALAR:])
+                for quarter in range(2):
+                    to = w1_to[:, quarter * (HALF // 2) : (quarter + 1) * (HALF // 2)]
+                    nc.vector.tensor_copy(to, w1_raw[1 + quarter][:].rearrange("p j (m t) -> p m j t", t=PACK))
             for t in range(PACK):
                 cols = slice(t * P + half * HALF, t * P + (half + 1) * HALF)
                 quantize(nc, w1_codes[:, cols], w1_scales[:, cols], grouped[:, t, :])
@@ -195,8 +195,8 @@ def tile_picked_pick_mlp_gelu_sub_e_kernel(tc, xT, w1, w2, offs, out):
         for s in range(2):
             bank = psum.tile([P, SLICE], F32, name=f"y_bank{s}")
             y_banks.append(bank)
-        y_fifth = psum.tile([P, GROUP], F32, name="y_fifth", tag="h_bank0")
-        y_sixth = psum.tile([P, GROUP], F32, name="y_sixth", tag="h_bank1")
+        y_late = psum.tile([P, GROUP + GROUP // 2], F32, name="y_late", tag="h_bank0")
+        y_last = psum.tile([P, GROUP // 2], F32, name="y_last", tag="h_bank1")
         for s in range(2):
             quantize_h(s * SLICE, SLICE)
             second_layer(y_banks[s][:], s * SLICE, SLICE)
@@ -204,11 +204,13 @@ def tile_picked_pick_mlp_gelu_sub_e_kernel(tc, xT, w1, w2, offs, out):
         nc.sync.dma_start(out=out[:, part(0)], in_=result[:, part(0)])
         nc.scalar.copy(result[:, part(1)], y_banks[1][:])
         nc.sync.dma_start(out=out[:, part(1)], in_=result[:, part(1)])
+        last = S - GROUP // 2
         quantize_h(4 * GROUP, GROUP)
-        second_layer(y_fifth[:], 4 * GROUP, GROUP)
-        nc.scalar.copy(result[:, 4 * GROUP : 5 * GROUP], y_fifth[:])
-        for start in (0, GROUP // 2):
-            quantize_h(5 * GROUP + start, GROUP // 2)
-            second_layer(y_sixth[:, start : start + GROUP // 2], 5 * GROUP + start, GROUP // 2)
-        nc.vector.tensor_copy(result[:, 5 * GROUP :], y_sixth[:])
+        second_layer(y_late[:, :GROUP], 4 * GROUP, GROUP)
+        quantize_h(5 * GROUP, GROUP // 2)
+        second_layer(y_late[:, GROUP:], 5 * GROUP, GROUP // 2)
+        nc.scalar.copy(result[:, 4 * GROUP : last], y_late[:])
+        quantize_h(last, GROUP // 2)
+        second_layer(y_last[:], last, GROUP // 2)
+        nc.vector.tensor_copy(result[:, last:], y_last[:])
         nc.sync.dma_start(out=out[:, part(2)], in_=result[:, part(2)])

@@ -46,9 +46,9 @@ def tile_picked_pick_mlp_gelu_sub_e_kernel(tc, xT, w1, w2, offs, out):
                 nc.sync.dma_start(offsets[:], offs)
         w1_rows = w1.rearrange("(p j) h -> p j h", j=PACK)
         w1_raw = []
-        for start, width in ((0, H // 2), (H // 2, H // 4), (3 * H // 4, H // 4)):
-            raw = keep.tile([P, PACK, width], F32, name=f"w1_raw{start}")
-            nc.sync.dma_start(out=raw[:], in_=w1_rows[:, :, start : start + width])
+        for quarter in range(4):
+            raw = keep.tile([P, PACK, P], F32, name=f"w1_raw{quarter}")
+            nc.sync.dma_start(out=raw[:], in_=w1_rows[:, :, quarter * P : (quarter + 1) * P])
             w1_raw.append(raw)
         w2_raw = keep.tile([P, PACK, N], F32, name="w2_raw")
         nc.sync.dma_start(out=w2_raw[:], in_=w2.rearrange("(p j) n -> p j n", j=PACK))
@@ -58,11 +58,16 @@ def tile_picked_pick_mlp_gelu_sub_e_kernel(tc, xT, w1, w2, offs, out):
         probe_out = keep.tile([P, 1], F32, name="probe_out")
         nc.scalar.activation(probe_out[:], probe[:], GELU)
 
-        picked = keep.tile([P, slices * (PACK - 1), SLICE], F32, name="picked")
-        x_grouped = []
-        for s in range(slices):
-            tile = keep.tile([P, SLICE, PACK], BF16, name=f"x_grouped{s}", align_bytes=ALIGN)
-            x_grouped.append(tile)
+        picked = keep.tile([P, 8, SLICE], F32, name="picked")
+        first_row = {2: 0, 0: 3, 1: 6}
+        piece = HALF * PACK
+        shared = keep.tile([P, piece + SLICE * PACK], BF16, name="shared", align_bytes=ALIGN)
+        x_flat = []
+        for s in range(slices - 1):
+            tile = keep.tile([P, SLICE * PACK], BF16, name=f"x_grouped{s}", align_bytes=ALIGN)
+            x_flat.append(tile[:])
+        x_flat.append(shared[:, piece:])
+        x_grouped = [flat.rearrange("p (n t) -> p n t", t=PACK) for flat in x_flat]
 
         def entries(s):
             return offsets[:, s * (SLICE // 16) : (s + 1) * (SLICE // 16)]
@@ -74,23 +79,25 @@ def tile_picked_pick_mlp_gelu_sub_e_kernel(tc, xT, w1, w2, offs, out):
             nc.vector.tensor_copy(x_grouped[s][:, :, j], planes[j][:].indirect(entries(s)))
 
         def gather_plain(j, s):
-            nc.vector.tensor_copy(picked[:, (PACK - 1) * s + j, :], planes[j][:].indirect(entries(s)))
+            nc.vector.tensor_copy(picked[:, first_row[s] + j, :], planes[j][:].indirect(entries(s)))
 
-        def interleave(s, count):
+        def interleave(s, first, count, tokens):
+            rows = slice(first_row[s] + first, first_row[s] + first + count)
             nc.scalar.copy(
-                x_grouped[s][:, :, :count].rearrange("p (c i) t -> p c t i", i=4),
-                picked[:, (PACK - 1) * s : (PACK - 1) * s + count, :].rearrange("p t (c i) -> p c t i", i=4),
+                x_grouped[s][:, tokens, first : first + count].rearrange("p (c i) t -> p c t i", i=4),
+                picked[:, rows, tokens].rearrange("p t (c i) -> p c t i", i=4),
             )
 
         for j in range(2):
             for s in range(slices):
                 gather_plain(j, s)
-        for s in range(1, slices):
-            interleave(s, 2)
+        for s in range(2):
+            interleave(s, 0, 2, slice(0, SLICE))
         gather_plain(2, 0)
-        interleave(0, PACK)
-        for s in range(1, slices):
-            gather_stepped(2, s)
+        interleave(0, 2, 2, slice(0, SLICE))
+        gather_plain(2, 2)
+        interleave(2, 0, PACK, slice(HALF, SLICE))
+        gather_stepped(2, 1)
         for s in range(slices - 1):
             gather_stepped(3, s)
 
@@ -98,32 +105,46 @@ def tile_picked_pick_mlp_gelu_sub_e_kernel(tc, xT, w1, w2, offs, out):
         x_scales = keep.tile([P, S], U8, name="x_scales", align_bytes=ALIGN)
 
         def quantize_x(codes, s):
-            quantize(nc, codes, x_scales[:, part(s)], x_grouped[s][:].rearrange("p n t -> p (n t)"))
+            quantize(nc, codes, x_scales[:, part(s)], x_flat[s])
 
         quantize_x(x_codes_first[:], 0)
 
         w1_codes = keep.tile([P, H], U32, name="w1_codes", align_bytes=ALIGN)
         w1_scales = keep.tile([P, H], U8, name="w1_scales", align_bytes=ALIGN)
-        for half in range(2):
-            grouped = late.tile(
-                [P, PACK, HALF * PACK], BF16, name=f"w1_grouped{half}", align_bytes=ALIGN, offset=half * 2048
-            )
-            w1_to = grouped[:].rearrange("p t (m j) -> p m j t", j=PACK)
-            if half == 0:
-                nc.scalar.copy(w1_to, w1_raw[0][:].rearrange("p j (m t) -> p m j t", t=PACK))
-            else:
-                for quarter in range(2):
-                    to = w1_to[:, quarter * (HALF // 2) : (quarter + 1) * (HALF // 2)]
-                    nc.vector.tensor_copy(to, w1_raw[1 + quarter][:].rearrange("p j (m t) -> p m j t", t=PACK))
-            for t in range(PACK):
-                cols = slice(t * P + half * HALF, t * P + (half + 1) * HALF)
-                quantize(nc, w1_codes[:, cols], w1_scales[:, cols], grouped[:, t, :])
+        w1_first = keep.tile([P, PACK, piece], BF16, name="w1_first", align_bytes=ALIGN)
+        w1_upper = late.tile([P, 2, piece], BF16, name="w1_upper", align_bytes=ALIGN, offset=0)
+        w1_lower = shared[:, : 2 * piece].rearrange("p (t c) -> p t c", t=2)
 
-        x_codes_second = late.tile([P, SLICE], U32, name="x_codes_second", align_bytes=ALIGN, offset=2048)
-        last_plane = late.tile([P, SLICE], F32, name="last_plane", align_bytes=ALIGN, offset=3072)
-        nc.vector.tensor_copy(last_plane[:], planes[3][:].indirect(entries(2)))
+        def w1_views(staged, quarter, tiles):
+            to = staged.rearrange("p t (m j) -> p m j t", j=PACK)
+            rows = slice(quarter % 2 * (HALF // 2), (quarter % 2 + 1) * (HALF // 2))
+            return to[:, rows], w1_raw[quarter][:].rearrange("p j (m t) -> p m j t", t=PACK)[:, :, :, tiles]
+
+        def quantize_w1(half, t, staged):
+            cols = slice(t * P + half * HALF, t * P + (half + 1) * HALF)
+            quantize(nc, w1_codes[:, cols], w1_scales[:, cols], staged)
+
+        for quarter in range(2):
+            nc.scalar.copy(*w1_views(w1_first[:], quarter, slice(0, PACK)))
+        for t in range(PACK):
+            quantize_w1(0, t, w1_first[:, t, :])
+        nc.vector.tensor_copy(*w1_views(w1_upper[:], 2, slice(2, PACK)))
+        nc.scalar.copy(*w1_views(w1_lower, 2, slice(0, 2)))
+        nc.scalar.copy(*w1_views(w1_lower, 3, slice(0, 2)))
+        nc.vector.tensor_copy(*w1_views(w1_upper[:], 3, slice(2, PACK)))
+        for t in range(2):
+            quantize_w1(1, 2 + t, w1_upper[:, t, :])
+        quantize_w1(1, 1, w1_lower[:, 1, :])
+        quantize_w1(1, 0, w1_lower[:, 0, :])
+
+        interleave(2, 0, PACK, slice(0, HALF))
+        x_codes_second = late.tile([P, SLICE], U32, name="x_codes_second", align_bytes=ALIGN, offset=0)
         quantize_x(x_codes_second[:], 1)
-        nc.vector.tensor_copy(x_grouped[2][:, :, 3], last_plane[:])
+        gather_stepped(3, 2)
+        w2_grouped = keep.tile([P, N, PACK], BF16, name="w2_grouped", align_bytes=ALIGN)
+        nc.vector.tensor_copy(
+            w2_grouped[:].rearrange("p (c i) t -> p c t i", i=4), w2_raw[:].rearrange("p t (c i) -> p c t i", i=4)
+        )
         x_codes_third = keep.tile([P, SLICE], U32, name="x_codes_third", align_bytes=ALIGN)
         quantize_x(x_codes_third[:], 2)
         x_tiles = [x_codes_first, x_codes_second, x_codes_third]
@@ -132,10 +153,6 @@ def tile_picked_pick_mlp_gelu_sub_e_kernel(tc, xT, w1, w2, offs, out):
             start = g * GROUP % SLICE
             return x_tiles[g * GROUP // SLICE][:, start : start + GROUP]
 
-        w2_grouped = keep.tile([P, N, PACK], BF16, name="w2_grouped", align_bytes=ALIGN)
-        nc.scalar.copy(
-            w2_grouped[:].rearrange("p (c i) t -> p c t i", i=4), w2_raw[:].rearrange("p t (c i) -> p c t i", i=4)
-        )
         w2_codes = keep.tile([P, N], U32, name="w2_codes", align_bytes=ALIGN)
         w2_scales = keep.tile([P, N], U8, name="w2_scales", align_bytes=ALIGN)
         quantize(nc, w2_codes[:], w2_scales[:], w2_grouped[:].rearrange("p n t -> p (n t)"))
@@ -147,11 +164,18 @@ def tile_picked_pick_mlp_gelu_sub_e_kernel(tc, xT, w1, w2, offs, out):
         for g in range(groups):
             bank = psum.tile([P, PACK, GROUP], F32, name=f"h_bank{g}")
             h_banks.append(bank)
-        h_grouped = keep.tile([P, S, PACK], BF16, name="h_grouped", align_bytes=ALIGN)
+        last = S - GROUP // 2
+        h_tiles = []
+        for s in range(slices):
+            tile = late.tile([P, SLICE, PACK], BF16, name=f"h_grouped{s}", align_bytes=ALIGN, offset=1024 + 2048 * s)
+            h_tiles.append(tile)
+
+        def h_grouped(start, width):
+            return h_tiles[start // SLICE][:, start % SLICE : start % SLICE + width, :]
 
         def first_layer(g):
             cols = slice(g * GROUP, (g + 1) * GROUP)
-            for t in range(PACK):
+            for t in (2, 3, 1, 0):
                 w_cols = slice(t * P, (t + 1) * P)
                 nc.tensor.matmul_mx(
                     out=h_banks[g][:, t, :],
@@ -164,14 +188,13 @@ def tile_picked_pick_mlp_gelu_sub_e_kernel(tc, xT, w1, w2, offs, out):
                 )
 
         def gelu(start, width):
-            cols = slice(start, start + width)
             own = slice(start % GROUP, start % GROUP + width)
             bank = h_banks[start // GROUP]
-            nc.scalar.activation(h_grouped[:, cols, :], bank[:, :, own].rearrange("p t n -> p n t"), GELU)
+            nc.scalar.activation(h_grouped(start, width), bank[:, :, own].rearrange("p t n -> p n t"), GELU)
 
         def quantize_h(start, width):
             cols = slice(start, start + width)
-            quantize(nc, h_codes[:, cols], h_scales[:, cols], h_grouped[:, cols, :].rearrange("p n t -> p (n t)"))
+            quantize(nc, h_codes[:, cols], h_scales[:, cols], h_grouped(start, width).rearrange("p n t -> p (n t)"))
 
         def second_layer(y, start, width):
             cols = slice(start, start + width)
@@ -185,26 +208,36 @@ def tile_picked_pick_mlp_gelu_sub_e_kernel(tc, xT, w1, w2, offs, out):
                 stop=True,
             )
 
+        y_banks = []
+        for s in range(2):
+            bank = psum.tile([P, SLICE], F32, name=f"y_bank{s}")
+            y_banks.append(bank)
+        for width in (SLICE, SLICE, SLICE):
+            nc.tensor.matmul_mx(
+                out=y_banks[0][:, :width],
+                lhsT=x_codes(0).bitcast(FP8X4),
+                lhsT_scale=x_scales[:, :GROUP],
+                rhs=x_codes_first[:, :width].bitcast(FP8X4),
+                rhs_scale=x_scales[:, :width],
+                start=True,
+                stop=True,
+            )
         for g in range(groups - 1):
             first_layer(g)
             gelu(g * GROUP, GROUP)
         first_layer(5)
         gelu(5 * GROUP, GROUP // 2)
         gelu(5 * GROUP + GROUP // 2, GROUP // 2)
-        y_banks = []
-        for s in range(2):
-            bank = psum.tile([P, SLICE], F32, name=f"y_bank{s}")
-            y_banks.append(bank)
         y_late = psum.tile([P, GROUP + GROUP // 2], F32, name="y_late", tag="h_bank0")
         y_last = psum.tile([P, GROUP // 2], F32, name="y_last", tag="h_bank1")
         for s in range(2):
             quantize_h(s * SLICE, SLICE)
             second_layer(y_banks[s][:], s * SLICE, SLICE)
-        nc.vector.tensor_copy(result[:, part(0)], y_banks[0][:])
-        nc.sync.dma_start(out=out[:, part(0)], in_=result[:, part(0)])
+        result_first = late.tile([P, SLICE], F32, name="result_first", align_bytes=ALIGN, offset=1024 + 2048)
+        nc.vector.tensor_copy(result_first[:], y_banks[0][:])
+        nc.sync.dma_start(out=out[:, part(0)], in_=result_first[:])
         nc.scalar.copy(result[:, part(1)], y_banks[1][:])
         nc.sync.dma_start(out=out[:, part(1)], in_=result[:, part(1)])
-        last = S - GROUP // 2
         quantize_h(4 * GROUP, GROUP)
         second_layer(y_late[:, :GROUP], 4 * GROUP, GROUP)
         quantize_h(5 * GROUP, GROUP // 2)

@@ -19,6 +19,7 @@ SLICE = 256
 GROUP = 128
 ALIGN = 64
 HALF = P // 2
+ORDER = (3, 0, 1, 2)
 
 
 def quantize(nc, codes, scales, values):
@@ -45,11 +46,11 @@ def tile_picked_pick_mlp_gelu_sub_e_kernel(tc, xT, w1, w2, offs, out):
             if j == 0:
                 nc.sync.dma_start(offsets[:], offs)
         w1_rows = w1.rearrange("(p j) h -> p j h", j=PACK)
-        w1_raw = []
-        for quarter in range(4):
-            raw = keep.tile([P, PACK, P], F32, name=f"w1_raw{quarter}")
-            nc.sync.dma_start(out=raw[:], in_=w1_rows[:, :, quarter * P : (quarter + 1) * P])
-            w1_raw.append(raw)
+        w1_pieces = []
+        for start, width in ((0, H // 2), (H // 2, H // 4), (3 * H // 4, H // 4)):
+            raw = late.tile([P, PACK, width], F32, name=f"w1_raw{start}", align_bytes=ALIGN, offset=16 * start)
+            nc.sync.dma_start(out=raw[:], in_=w1_rows[:, :, start : start + width])
+            w1_pieces.append((start, width, raw))
         w2_raw = keep.tile([P, PACK, N], F32, name="w2_raw")
         nc.sync.dma_start(out=w2_raw[:], in_=w2.rearrange("(p j) n -> p j n", j=PACK))
 
@@ -60,13 +61,13 @@ def tile_picked_pick_mlp_gelu_sub_e_kernel(tc, xT, w1, w2, offs, out):
 
         picked = keep.tile([P, 8, SLICE], F32, name="picked")
         first_row = {2: 0, 0: 3, 1: 6}
-        piece = HALF * PACK
-        shared = keep.tile([P, piece + SLICE * PACK], BF16, name="shared", align_bytes=ALIGN)
+        x_start = (PACK - 1) * HALF * PACK
+        shared = keep.tile([P, x_start + SLICE * PACK], BF16, name="shared", align_bytes=ALIGN)
         x_flat = []
         for s in range(slices - 1):
             tile = keep.tile([P, SLICE * PACK], BF16, name=f"x_grouped{s}", align_bytes=ALIGN)
             x_flat.append(tile[:])
-        x_flat.append(shared[:, piece:])
+        x_flat.append(shared[:, x_start:])
         x_grouped = [flat.rearrange("p (n t) -> p n t", t=PACK) for flat in x_flat]
 
         def entries(s):
@@ -111,35 +112,26 @@ def tile_picked_pick_mlp_gelu_sub_e_kernel(tc, xT, w1, w2, offs, out):
 
         w1_codes = keep.tile([P, H], U32, name="w1_codes", align_bytes=ALIGN)
         w1_scales = keep.tile([P, H], U8, name="w1_scales", align_bytes=ALIGN)
-        w1_first = keep.tile([P, PACK, piece], BF16, name="w1_first", align_bytes=ALIGN)
-        w1_upper = late.tile([P, 2, piece], BF16, name="w1_upper", align_bytes=ALIGN, offset=0)
-        w1_lower = shared[:, : 2 * piece].rearrange("p (t c) -> p t c", t=2)
+        x_hold = 16384
+        w1_first = late.tile([P, PACK, HALF * PACK], BF16, name="w1_first", align_bytes=ALIGN, offset=x_hold)
+        w1_halves = [w1_first[:], shared[:, : HALF * PACK * PACK].rearrange("p (t c) -> p t c", t=PACK)]
 
-        def w1_views(staged, quarter, tiles):
-            to = staged.rearrange("p t (m j) -> p m j t", j=PACK)
-            rows = slice(quarter % 2 * (HALF // 2), (quarter % 2 + 1) * (HALF // 2))
-            return to[:, rows], w1_raw[quarter][:].rearrange("p j (m t) -> p m j t", t=PACK)[:, :, :, tiles]
+        def quantize_w1(half):
+            for t in ORDER:
+                cols = slice(t * P + half * HALF, t * P + (half + 1) * HALF)
+                quantize(nc, w1_codes[:, cols], w1_scales[:, cols], w1_halves[half][:, t, :])
 
-        def quantize_w1(half, t, staged):
-            cols = slice(t * P + half * HALF, t * P + (half + 1) * HALF)
-            quantize(nc, w1_codes[:, cols], w1_scales[:, cols], staged)
-
-        for quarter in range(2):
-            nc.scalar.copy(*w1_views(w1_first[:], quarter, slice(0, PACK)))
-        for t in range(PACK):
-            quantize_w1(0, t, w1_first[:, t, :])
-        nc.vector.tensor_copy(*w1_views(w1_upper[:], 2, slice(2, PACK)))
-        nc.scalar.copy(*w1_views(w1_lower, 2, slice(0, 2)))
-        nc.scalar.copy(*w1_views(w1_lower, 3, slice(0, 2)))
-        nc.vector.tensor_copy(*w1_views(w1_upper[:], 3, slice(2, PACK)))
-        for t in range(2):
-            quantize_w1(1, 2 + t, w1_upper[:, t, :])
-        quantize_w1(1, 1, w1_lower[:, 1, :])
-        quantize_w1(1, 0, w1_lower[:, 0, :])
+        for start, width, raw in w1_pieces:
+            half, row = divmod(start // PACK, HALF)
+            to = w1_halves[half].rearrange("p t (m j) -> p m j t", j=PACK)[:, row : row + width // PACK]
+            copy = nc.scalar.copy if half == 0 else nc.vector.tensor_copy
+            copy(to, raw[:].rearrange("p j (m t) -> p m j t", t=PACK))
+        quantize_w1(0)
+        quantize_w1(1)
+        x_codes_second = late.tile([P, SLICE], U32, name="x_codes_second", align_bytes=ALIGN, offset=x_hold)
+        quantize_x(x_codes_second[:], 1)
 
         interleave(2, 0, PACK, slice(0, HALF))
-        x_codes_second = late.tile([P, SLICE], U32, name="x_codes_second", align_bytes=ALIGN, offset=0)
-        quantize_x(x_codes_second[:], 1)
         gather_stepped(3, 2)
         w2_grouped = keep.tile([P, N, PACK], BF16, name="w2_grouped", align_bytes=ALIGN)
         nc.vector.tensor_copy(
@@ -167,7 +159,7 @@ def tile_picked_pick_mlp_gelu_sub_e_kernel(tc, xT, w1, w2, offs, out):
         last = S - GROUP // 2
         h_tiles = []
         for s in range(slices):
-            tile = late.tile([P, SLICE, PACK], BF16, name=f"h_grouped{s}", align_bytes=ALIGN, offset=1024 + 2048 * s)
+            tile = late.tile([P, SLICE, PACK], BF16, name=f"h_grouped{s}", align_bytes=ALIGN, offset=8192 + 2048 * s)
             h_tiles.append(tile)
 
         def h_grouped(start, width):
@@ -175,7 +167,7 @@ def tile_picked_pick_mlp_gelu_sub_e_kernel(tc, xT, w1, w2, offs, out):
 
         def first_layer(g):
             cols = slice(g * GROUP, (g + 1) * GROUP)
-            for t in (2, 3, 1, 0):
+            for t in ORDER:
                 w_cols = slice(t * P, (t + 1) * P)
                 nc.tensor.matmul_mx(
                     out=h_banks[g][:, t, :],
@@ -233,7 +225,7 @@ def tile_picked_pick_mlp_gelu_sub_e_kernel(tc, xT, w1, w2, offs, out):
         for s in range(2):
             quantize_h(s * SLICE, SLICE)
             second_layer(y_banks[s][:], s * SLICE, SLICE)
-        result_first = late.tile([P, SLICE], F32, name="result_first", align_bytes=ALIGN, offset=1024 + 2048)
+        result_first = late.tile([P, SLICE], F32, name="result_first", align_bytes=ALIGN, offset=8192 + 2048)
         nc.vector.tensor_copy(result_first[:], y_banks[0][:])
         nc.sync.dma_start(out=out[:, part(0)], in_=result_first[:])
         nc.scalar.copy(result[:, part(1)], y_banks[1][:])

@@ -19,7 +19,7 @@ SLICE = 256
 GROUP = 128
 ALIGN = 64
 HALF = P // 2
-ORDER = (3, 0, 1, 2)
+ORDER = (2, 3, 0, 1)
 
 
 def quantize(nc, codes, scales, values):
@@ -46,11 +46,11 @@ def tile_picked_pick_mlp_gelu_sub_e_kernel(tc, xT, w1, w2, offs, out):
             if j == 0:
                 nc.sync.dma_start(offsets[:], offs)
         w1_rows = w1.rearrange("(p j) h -> p j h", j=PACK)
-        w1_pieces = []
-        for start, width in ((0, H // 2), (H // 2, H // 4), (3 * H // 4, H // 4)):
-            raw = late.tile([P, PACK, width], F32, name=f"w1_raw{start}", align_bytes=ALIGN, offset=16 * start)
-            nc.sync.dma_start(out=raw[:], in_=w1_rows[:, :, start : start + width])
-            w1_pieces.append((start, width, raw))
+        w1_raw = []
+        for pair in range(2):
+            raw = keep.tile([P, 2, H], F32, name=f"w1_raw{pair}")
+            nc.sync.dma_start(out=raw[:], in_=w1_rows[:, 2 * pair : 2 * pair + 2, :])
+            w1_raw.append(raw)
         w2_raw = keep.tile([P, PACK, N], F32, name="w2_raw")
         nc.sync.dma_start(out=w2_raw[:], in_=w2.rearrange("(p j) n -> p j n", j=PACK))
 
@@ -61,7 +61,7 @@ def tile_picked_pick_mlp_gelu_sub_e_kernel(tc, xT, w1, w2, offs, out):
 
         picked = keep.tile([P, 8, SLICE], F32, name="picked")
         first_row = {2: 0, 0: 3, 1: 6}
-        x_start = (PACK - 1) * HALF * PACK
+        x_start = 2 * H - HALF * PACK
         shared = keep.tile([P, x_start + SLICE * PACK], BF16, name="shared", align_bytes=ALIGN)
         x_flat = []
         for s in range(slices - 1):
@@ -112,28 +112,31 @@ def tile_picked_pick_mlp_gelu_sub_e_kernel(tc, xT, w1, w2, offs, out):
 
         w1_codes = keep.tile([P, H], U32, name="w1_codes", align_bytes=ALIGN)
         w1_scales = keep.tile([P, H], U8, name="w1_scales", align_bytes=ALIGN)
-        x_hold = 16384
-        w1_first = late.tile([P, PACK, HALF * PACK], BF16, name="w1_first", align_bytes=ALIGN, offset=x_hold)
-        w1_halves = [w1_first[:], shared[:, : HALF * PACK * PACK].rearrange("p (t c) -> p t c", t=PACK)]
+        w1_lower = late.tile([P, 2, H], BF16, name="w1_lower", align_bytes=ALIGN, offset=0)
+        w1_grouped = [w1_lower[:], shared[:, : 2 * H].rearrange("p (t c) -> p t c", t=2)]
 
-        def quantize_w1(half):
-            for t in ORDER:
-                cols = slice(t * P + half * HALF, t * P + (half + 1) * HALF)
-                quantize(nc, w1_codes[:, cols], w1_scales[:, cols], w1_halves[half][:, t, :])
 
-        for start, width, raw in w1_pieces:
-            half, row = divmod(start // PACK, HALF)
-            to = w1_halves[half].rearrange("p t (m j) -> p m j t", j=PACK)[:, row : row + width // PACK]
-            copy = nc.scalar.copy if half == 0 else nc.vector.tensor_copy
-            copy(to, raw[:].rearrange("p j (m t) -> p m j t", t=PACK))
-        quantize_w1(0)
-        quantize_w1(1)
-        x_codes_second = late.tile([P, SLICE], U32, name="x_codes_second", align_bytes=ALIGN, offset=x_hold)
+        def lay_out(copy, pair, first, count):
+            to = w1_grouped[first // 2].rearrange("p t (m j) -> p m j t", j=PACK)
+            copy(
+                to[:, :, 2 * pair : 2 * pair + 2, first % 2 : first % 2 + count],
+                w1_raw[pair][:].rearrange("p j (m t) -> p m j t", t=PACK)[:, :, :, first : first + count],
+            )
+
+        lay_out(nc.scalar.copy, 0, 0, 2)
+        lay_out(nc.vector.tensor_copy, 0, 2, 2)
+        lay_out(nc.scalar.copy, 1, 0, 2)
+        for t in (2, 3):
+            lay_out(nc.vector.tensor_copy, 1, t, 1)
+        for t in ORDER:
+            cols = slice(t * P, (t + 1) * P)
+            quantize(nc, w1_codes[:, cols], w1_scales[:, cols], w1_grouped[t // 2][:, t % 2, :])
+        x_codes_second = late.tile([P, SLICE], U32, name="x_codes_second", align_bytes=ALIGN, offset=0)
         quantize_x(x_codes_second[:], 1)
 
         interleave(2, 0, PACK, slice(0, HALF))
         gather_stepped(3, 2)
-        w2_grouped = keep.tile([P, N, PACK], BF16, name="w2_grouped", align_bytes=ALIGN)
+        w2_grouped = late.tile([P, N, PACK], BF16, name="w2_grouped", align_bytes=ALIGN, offset=1024)
         nc.vector.tensor_copy(
             w2_grouped[:].rearrange("p (c i) t -> p c t i", i=4), w2_raw[:].rearrange("p t (c i) -> p c t i", i=4)
         )

@@ -47,9 +47,9 @@ def tile_picked_pick_mlp_gelu_sub_e_kernel(tc, xT, w1, w2, offs, out):
                 nc.sync.dma_start(offsets[:], offs)
         w1_rows = w1.rearrange("(p j) h -> p j h", j=PACK)
         w1_raw = []
-        for pair in range(2):
-            raw = keep.tile([P, 2, H], F32, name=f"w1_raw{pair}")
-            nc.sync.dma_start(out=raw[:], in_=w1_rows[:, 2 * pair : 2 * pair + 2, :])
+        for half in range(2):
+            raw = keep.tile([P, PACK, H // 2], F32, name=f"w1_raw{half}")
+            nc.sync.dma_start(out=raw[:], in_=w1_rows[:, :, half * (H // 2) : (half + 1) * (H // 2)])
             w1_raw.append(raw)
         w2_raw = keep.tile([P, PACK, N], F32, name="w2_raw")
         nc.sync.dma_start(out=w2_raw[:], in_=w2.rearrange("(p j) n -> p j n", j=PACK))
@@ -61,7 +61,7 @@ def tile_picked_pick_mlp_gelu_sub_e_kernel(tc, xT, w1, w2, offs, out):
 
         picked = keep.tile([P, 8, SLICE], F32, name="picked")
         first_row = {2: 0, 0: 3, 1: 6}
-        x_start = 2 * H - HALF * PACK
+        x_start = HALF * PACK
         shared = keep.tile([P, x_start + SLICE * PACK], BF16, name="shared", align_bytes=ALIGN)
         x_flat = []
         for s in range(slices - 1):
@@ -112,25 +112,31 @@ def tile_picked_pick_mlp_gelu_sub_e_kernel(tc, xT, w1, w2, offs, out):
 
         w1_codes = keep.tile([P, H], U32, name="w1_codes", align_bytes=ALIGN)
         w1_scales = keep.tile([P, H], U8, name="w1_scales", align_bytes=ALIGN)
-        w1_lower = late.tile([P, 2, H], BF16, name="w1_lower", align_bytes=ALIGN, offset=0)
-        w1_grouped = [w1_lower[:], shared[:, : 2 * H].rearrange("p (t c) -> p t c", t=2)]
+        w1_first = keep.tile([P, PACK, HALF * PACK], BF16, name="w1_first", align_bytes=ALIGN)
+        w1_lower = late.tile([P, 2, HALF * PACK], BF16, name="w1_lower", align_bytes=ALIGN, offset=512)
+        w1_upper = shared[:, : 2 * HALF * PACK].rearrange("p (t c) -> p t c", t=2)
+        w1_grouped = [[w1_first[:, :2], w1_first[:, 2:]], [w1_lower[:], w1_upper]]
 
-
-        def lay_out(copy, pair, first, count):
-            to = w1_grouped[first // 2].rearrange("p t (m j) -> p m j t", j=PACK)
+        def lay_out(copy, half, side):
             copy(
-                to[:, :, 2 * pair : 2 * pair + 2, first % 2 : first % 2 + count],
-                w1_raw[pair][:].rearrange("p j (m t) -> p m j t", t=PACK)[:, :, :, first : first + count],
+                w1_grouped[half][side].rearrange("p t (m j) -> p m j t", j=PACK),
+                w1_raw[half][:].rearrange("p j (m t) -> p m j t", t=PACK)[:, :, :, 2 * side : 2 * side + 2],
             )
 
-        lay_out(nc.scalar.copy, 0, 0, 2)
-        lay_out(nc.vector.tensor_copy, 0, 2, 2)
-        lay_out(nc.scalar.copy, 1, 0, 2)
-        for t in (2, 3):
-            lay_out(nc.vector.tensor_copy, 1, t, 1)
-        for t in ORDER:
-            cols = slice(t * P, (t + 1) * P)
-            quantize(nc, w1_codes[:, cols], w1_scales[:, cols], w1_grouped[t // 2][:, t % 2, :])
+        def quantize_w1(half, side):
+            for e in range(2):
+                start = (2 * side + e) * P + half * HALF
+                cols = slice(start, start + HALF)
+                quantize(nc, w1_codes[:, cols], w1_scales[:, cols], w1_grouped[half][side][:, e, :])
+
+        for side in range(2):
+            lay_out(nc.scalar.copy, 0, side)
+        lay_out(nc.scalar.copy, 1, 0)
+        quantize_w1(0, 0)
+        lay_out(nc.vector.tensor_copy, 1, 1)
+        quantize_w1(0, 1)
+        quantize_w1(1, 1)
+        quantize_w1(1, 0)
         x_codes_second = late.tile([P, SLICE], U32, name="x_codes_second", align_bytes=ALIGN, offset=0)
         quantize_x(x_codes_second[:], 1)
 
@@ -207,16 +213,6 @@ def tile_picked_pick_mlp_gelu_sub_e_kernel(tc, xT, w1, w2, offs, out):
         for s in range(2):
             bank = psum.tile([P, SLICE], F32, name=f"y_bank{s}")
             y_banks.append(bank)
-        for width in (SLICE, SLICE, SLICE):
-            nc.tensor.matmul_mx(
-                out=y_banks[0][:, :width],
-                lhsT=x_codes(0).bitcast(FP8X4),
-                lhsT_scale=x_scales[:, :GROUP],
-                rhs=x_codes_first[:, :width].bitcast(FP8X4),
-                rhs_scale=x_scales[:, :width],
-                start=True,
-                stop=True,
-            )
         for g in range(groups - 1):
             first_layer(g)
             gelu(g * GROUP, GROUP)

@@ -17,13 +17,26 @@ P = 128
 PACK = 4
 SLICE = 256
 GROUP = 128
+HALF = 64
 ALIGN = 64
-HALF = P // 2
-ORDER = (2, 3, 0, 1)
+SIDES = (1, 0)
+STAGED = HALF * PACK
 
 
 def quantize(nc, codes, scales, values):
     nc.vector.quantize_mx(out=codes.bitcast(FP8X4), scales=scales, in_=values)
+
+
+def multiply(nc, product, weights, weight_scales, tokens, token_scales):
+    nc.tensor.matmul_mx(
+        out=product,
+        lhsT=weights.bitcast(FP8X4),
+        lhsT_scale=weight_scales,
+        rhs=tokens.bitcast(FP8X4),
+        rhs_scale=token_scales,
+        start=True,
+        stop=True,
+    )
 
 
 def tile_picked_pick_mlp_gelu_sub_e_kernel(tc, xT, w1, w2, offs, out):
@@ -33,7 +46,7 @@ def tile_picked_pick_mlp_gelu_sub_e_kernel(tc, xT, w1, w2, offs, out):
 
     with ExitStack() as ctx:
         keep = ctx.enter_context(tc.tile_pool(name="keep", bufs=1))
-        late = ctx.enter_context(tc.tile_pool(name="late", bufs=1))
+        reused = ctx.enter_context(tc.tile_pool(name="reused", bufs=1))
         psum = ctx.enter_context(tc.psum_pool(name="psum", bufs=1))
 
         offsets = keep.tile([P, S // 16], U16, name="offsets")
@@ -46,29 +59,31 @@ def tile_picked_pick_mlp_gelu_sub_e_kernel(tc, xT, w1, w2, offs, out):
             if j == 0:
                 nc.sync.dma_start(offsets[:], offs)
         w1_rows = w1.rearrange("(p j) h -> p j h", j=PACK)
-        w1_raw = []
-        for half in range(2):
-            raw = keep.tile([P, PACK, H // 2], F32, name=f"w1_raw{half}")
-            nc.sync.dma_start(out=raw[:], in_=w1_rows[:, :, half * (H // 2) : (half + 1) * (H // 2)])
-            w1_raw.append(raw)
+        w1_pieces = []
+        for start, width in ((0, H // 2), (H // 2, H // 4), (3 * H // 4, H // 4)):
+            raw = keep.tile([P, PACK, width], F32, name=f"w1_raw{start}")
+            nc.sync.dma_start(out=raw[:], in_=w1_rows[:, :, start : start + width])
+            w1_pieces.append(raw[:].rearrange("p j (a u b e) -> p u a j b e", u=2, b=2, e=2))
         w2_raw = keep.tile([P, PACK, N], F32, name="w2_raw")
-        nc.sync.dma_start(out=w2_raw[:], in_=w2.rearrange("(p j) n -> p j n", j=PACK))
+        w2_rows = w2.rearrange("(a u b e) n -> b a u (e n)", u=2, b=2, e=2)
+        for b in range(2):
+            nc.sync.dma_start(out=w2_raw[b::2].rearrange("p (u e) n -> p u (e n)", u=2), in_=w2_rows[b])
 
-        probe = keep.tile([P, 1], F32, name="probe")
-        nc.vector.memset(probe[:], 0.0)
-        probe_out = keep.tile([P, 1], F32, name="probe_out")
-        nc.scalar.activation(probe_out[:], probe[:], GELU)
+        table_in = keep.tile([P, 1], F32, name="table_in")
+        nc.vector.memset(table_in[:], 0.0)
+        table_out = keep.tile([P, 1], F32, name="table_out")
+        nc.scalar.activation(table_out[:], table_in[:], GELU)
+
+        shared = keep.tile([P, STAGED + SLICE * PACK], BF16, name="shared", align_bytes=ALIGN)
+        x_flat = []
+        for s in range(slices - 1):
+            tile = keep.tile([P, SLICE * PACK], BF16, name=f"x_staged{s}", align_bytes=ALIGN)
+            x_flat.append(tile[:])
+        x_flat.append(shared[:, STAGED:])
+        x_staged = [flat.rearrange("p (n j) -> p n j", j=PACK) for flat in x_flat]
 
         picked = keep.tile([P, 8, SLICE], F32, name="picked")
         first_row = {2: 0, 0: 3, 1: 6}
-        x_start = HALF * PACK
-        shared = keep.tile([P, x_start + SLICE * PACK], BF16, name="shared", align_bytes=ALIGN)
-        x_flat = []
-        for s in range(slices - 1):
-            tile = keep.tile([P, SLICE * PACK], BF16, name=f"x_grouped{s}", align_bytes=ALIGN)
-            x_flat.append(tile[:])
-        x_flat.append(shared[:, x_start:])
-        x_grouped = [flat.rearrange("p (n t) -> p n t", t=PACK) for flat in x_flat]
 
         def entries(s):
             return offsets[:, s * (SLICE // 16) : (s + 1) * (SLICE // 16)]
@@ -76,165 +91,139 @@ def tile_picked_pick_mlp_gelu_sub_e_kernel(tc, xT, w1, w2, offs, out):
         def part(s):
             return slice(s * SLICE, (s + 1) * SLICE)
 
-        def gather_stepped(j, s):
-            nc.vector.tensor_copy(x_grouped[s][:, :, j], planes[j][:].indirect(entries(s)))
+        def gather_into_place(j, s):
+            nc.vector.tensor_copy(x_staged[s][:, :, j], planes[j][:].indirect(entries(s)))
 
         def gather_plain(j, s):
             nc.vector.tensor_copy(picked[:, first_row[s] + j, :], planes[j][:].indirect(entries(s)))
 
-        def interleave(s, first, count, tokens):
-            rows = slice(first_row[s] + first, first_row[s] + first + count)
+        def interleave(s, places, tokens):
+            rows = slice(first_row[s] + places.start, first_row[s] + places.stop)
             nc.scalar.copy(
-                x_grouped[s][:, tokens, first : first + count].rearrange("p (c i) t -> p c t i", i=4),
-                picked[:, rows, tokens].rearrange("p t (c i) -> p c t i", i=4),
+                x_staged[s][:, tokens, places].rearrange("p (c i) j -> p c j i", i=4),
+                picked[:, rows, tokens].rearrange("p j (c i) -> p c j i", i=4),
             )
 
+        whole = slice(0, SLICE)
         for j in range(2):
             for s in range(slices):
                 gather_plain(j, s)
         for s in range(2):
-            interleave(s, 0, 2, slice(0, SLICE))
+            interleave(s, slice(0, 2), whole)
         gather_plain(2, 0)
-        interleave(0, 2, 2, slice(0, SLICE))
+        interleave(0, slice(2, PACK), whole)
         gather_plain(2, 2)
-        interleave(2, 0, PACK, slice(HALF, SLICE))
-        gather_stepped(2, 1)
-        for s in range(slices - 1):
-            gather_stepped(3, s)
+        interleave(2, slice(0, PACK), slice(HALF, SLICE))
+        gather_into_place(2, 1)
+        for s in range(2):
+            gather_into_place(3, s)
 
-        x_codes_first = keep.tile([P, SLICE], U32, name="x_codes_first", align_bytes=ALIGN)
         x_scales = keep.tile([P, S], U8, name="x_scales", align_bytes=ALIGN)
+        x_codes = []
 
         def quantize_x(codes, s):
-            quantize(nc, codes, x_scales[:, part(s)], x_flat[s])
+            quantize(nc, codes[:], x_scales[:, part(s)], x_flat[s])
+            x_codes.append(codes)
 
-        quantize_x(x_codes_first[:], 0)
+        quantize_x(keep.tile([P, SLICE], U32, name="x_codes0", align_bytes=ALIGN), 0)
 
         w1_codes = keep.tile([P, H], U32, name="w1_codes", align_bytes=ALIGN)
         w1_scales = keep.tile([P, H], U8, name="w1_scales", align_bytes=ALIGN)
-        w1_first = keep.tile([P, PACK, HALF * PACK], BF16, name="w1_first", align_bytes=ALIGN)
-        w1_lower = late.tile([P, 2, HALF * PACK], BF16, name="w1_lower", align_bytes=ALIGN, offset=512)
-        w1_upper = shared[:, : 2 * HALF * PACK].rearrange("p (t c) -> p t c", t=2)
-        w1_grouped = [[w1_first[:, :2], w1_first[:, 2:]], [w1_lower[:], w1_upper]]
+        w1_first = keep.tile([P, PACK, STAGED], BF16, name="w1_first", align_bytes=ALIGN)
+        w1_last = reused.tile([P, 2, STAGED], BF16, name="w1_last", align_bytes=ALIGN, offset=512)
+        w1_shared = shared[:, : 2 * STAGED].rearrange("p (e c) -> p e c", e=2)
+        w1_staged = [[w1_first[:, :2], w1_first[:, 2:]], [w1_last[:], w1_shared]]
 
-        def lay_out(copy, half, side):
-            copy(
-                w1_grouped[half][side].rearrange("p t (m j) -> p m j t", j=PACK),
-                w1_raw[half][:].rearrange("p j (m t) -> p m j t", t=PACK)[:, :, :, 2 * side : 2 * side + 2],
-            )
+        def lay_out(copy, piece, half, rows, u):
+            to = w1_staged[half][u].rearrange("p e (a b j) -> p a j b e", b=2, j=PACK)
+            copy(to[:, rows], w1_pieces[piece][:, u])
 
-        def quantize_w1(half, side):
-            for e in range(2):
-                start = (2 * side + e) * P + half * HALF
-                cols = slice(start, start + HALF)
-                quantize(nc, w1_codes[:, cols], w1_scales[:, cols], w1_grouped[half][side][:, e, :])
+        quarter = HALF // 4
+        for u in SIDES:
+            lay_out(nc.scalar.copy, 0, 0, slice(0, 2 * quarter), u)
+        for u in range(2):
+            lay_out(nc.vector.tensor_copy, 1, 1, slice(0, quarter), u)
+        lay_out(nc.scalar.copy, 2, 1, slice(quarter, 2 * quarter), 0)
+        lay_out(nc.vector.tensor_copy, 2, 1, slice(quarter, 2 * quarter), 1)
+        for half in range(2):
+            for u in SIDES:
+                for e in range(2):
+                    start = (2 * u + e) * P + half * HALF
+                    cols = slice(start, start + HALF)
+                    quantize(nc, w1_codes[:, cols], w1_scales[:, cols], w1_staged[half][u][:, e, :])
 
-        for side in range(2):
-            lay_out(nc.scalar.copy, 0, side)
-        lay_out(nc.scalar.copy, 1, 0)
-        quantize_w1(0, 0)
-        lay_out(nc.vector.tensor_copy, 1, 1)
-        quantize_w1(0, 1)
-        quantize_w1(1, 1)
-        quantize_w1(1, 0)
-        x_codes_second = late.tile([P, SLICE], U32, name="x_codes_second", align_bytes=ALIGN, offset=0)
-        quantize_x(x_codes_second[:], 1)
-
-        interleave(2, 0, PACK, slice(0, HALF))
-        gather_stepped(3, 2)
-        w2_grouped = late.tile([P, N, PACK], BF16, name="w2_grouped", align_bytes=ALIGN, offset=1024)
+        quantize_x(reused.tile([P, SLICE], U32, name="x_codes1", align_bytes=ALIGN, offset=0), 1)
+        interleave(2, slice(0, PACK), slice(0, HALF))
+        gather_into_place(3, 2)
+        w2_staged = reused.tile([P, N, PACK], BF16, name="w2_staged", align_bytes=ALIGN, offset=1024)
         nc.vector.tensor_copy(
-            w2_grouped[:].rearrange("p (c i) t -> p c t i", i=4), w2_raw[:].rearrange("p t (c i) -> p c t i", i=4)
+            w2_staged[:].rearrange("p (c i) t -> p c t i", i=4), w2_raw[:].rearrange("p t (c i) -> p c t i", i=4)
         )
-        x_codes_third = keep.tile([P, SLICE], U32, name="x_codes_third", align_bytes=ALIGN)
-        quantize_x(x_codes_third[:], 2)
-        x_tiles = [x_codes_first, x_codes_second, x_codes_third]
-
-        def x_codes(g):
-            start = g * GROUP % SLICE
-            return x_tiles[g * GROUP // SLICE][:, start : start + GROUP]
-
+        quantize_x(keep.tile([P, SLICE], U32, name="x_codes2", align_bytes=ALIGN), 2)
         w2_codes = keep.tile([P, N], U32, name="w2_codes", align_bytes=ALIGN)
         w2_scales = keep.tile([P, N], U8, name="w2_scales", align_bytes=ALIGN)
-        quantize(nc, w2_codes[:], w2_scales[:], w2_grouped[:].rearrange("p n t -> p (n t)"))
+        quantize(nc, w2_codes[:], w2_scales[:], w2_staged[:].rearrange("p n t -> p (n t)"))
 
-        h_codes = keep.tile([P, S], U32, name="h_codes", align_bytes=ALIGN)
-        h_scales = keep.tile([P, S], U8, name="h_scales", align_bytes=ALIGN)
-        result = keep.tile([P, S], F32, name="result")
+        h_offset, h_bytes = 2048, SLICE * PACK * 2
+        h_staged = []
+        for s in range(slices):
+            tile = reused.tile(
+                [P, SLICE, PACK], BF16, name=f"h_staged{s}", align_bytes=ALIGN, offset=h_offset + s * h_bytes
+            )
+            h_staged.append(tile)
         h_banks = []
         for g in range(groups):
             bank = psum.tile([P, PACK, GROUP], F32, name=f"h_bank{g}")
             h_banks.append(bank)
-        last = S - GROUP // 2
-        h_tiles = []
-        for s in range(slices):
-            tile = late.tile([P, SLICE, PACK], BF16, name=f"h_grouped{s}", align_bytes=ALIGN, offset=8192 + 2048 * s)
-            h_tiles.append(tile)
 
-        def h_grouped(start, width):
-            return h_tiles[start // SLICE][:, start % SLICE : start % SLICE + width, :]
-
-        def first_layer(g):
-            cols = slice(g * GROUP, (g + 1) * GROUP)
-            for t in ORDER:
-                w_cols = slice(t * P, (t + 1) * P)
-                nc.tensor.matmul_mx(
-                    out=h_banks[g][:, t, :],
-                    lhsT=w1_codes[:, w_cols].bitcast(FP8X4),
-                    lhsT_scale=w1_scales[:, w_cols],
-                    rhs=x_codes(g).bitcast(FP8X4),
-                    rhs_scale=x_scales[:, cols],
-                    start=True,
-                    stop=True,
-                )
+        def h_values(start, width):
+            return h_staged[start // SLICE][:, start % SLICE : start % SLICE + width, :]
 
         def gelu(start, width):
             own = slice(start % GROUP, start % GROUP + width)
             bank = h_banks[start // GROUP]
-            nc.scalar.activation(h_grouped(start, width), bank[:, :, own].rearrange("p t n -> p n t"), GELU)
+            nc.scalar.activation(h_values(start, width), bank[:, :, own].rearrange("p t n -> p n t"), GELU)
 
-        def quantize_h(start, width):
-            cols = slice(start, start + width)
-            quantize(nc, h_codes[:, cols], h_scales[:, cols], h_grouped(start, width).rearrange("p n t -> p (n t)"))
+        last = S - HALF
+        for g in range(groups):
+            start = g * GROUP
+            tokens = x_codes[start // SLICE][:, start % SLICE : start % SLICE + GROUP]
+            for u in SIDES:
+                for t in (2 * u, 2 * u + 1):
+                    cols = slice(t * P, (t + 1) * P)
+                    token_scales = x_scales[:, start : start + GROUP]
+                    multiply(nc, h_banks[g][:, t, :], w1_codes[:, cols], w1_scales[:, cols], tokens, token_scales)
+            if g < groups - 1:
+                gelu(start, GROUP)
+        gelu(last - HALF, HALF)
+        gelu(last, HALF)
 
-        def second_layer(y, start, width):
+        h_codes = keep.tile([P, S], U32, name="h_codes", align_bytes=ALIGN)
+        h_scales = keep.tile([P, S], U8, name="h_scales", align_bytes=ALIGN)
+
+        def second_product(y, start, width):
             cols = slice(start, start + width)
-            nc.tensor.matmul_mx(
-                out=y,
-                lhsT=w2_codes[:].bitcast(FP8X4),
-                lhsT_scale=w2_scales[:],
-                rhs=h_codes[:, cols].bitcast(FP8X4),
-                rhs_scale=h_scales[:, cols],
-                start=True,
-                stop=True,
-            )
+            quantize(nc, h_codes[:, cols], h_scales[:, cols], h_values(start, width).rearrange("p n t -> p (n t)"))
+            multiply(nc, y, w2_codes[:], w2_scales[:], h_codes[:, cols], h_scales[:, cols])
 
         y_banks = []
         for s in range(2):
             bank = psum.tile([P, SLICE], F32, name=f"y_bank{s}")
+            second_product(bank[:], s * SLICE, SLICE)
             y_banks.append(bank)
-        for g in range(groups - 1):
-            first_layer(g)
-            gelu(g * GROUP, GROUP)
-        first_layer(5)
-        gelu(5 * GROUP, GROUP // 2)
-        gelu(5 * GROUP + GROUP // 2, GROUP // 2)
-        y_late = psum.tile([P, GROUP + GROUP // 2], F32, name="y_late", tag="h_bank0")
-        y_last = psum.tile([P, GROUP // 2], F32, name="y_last", tag="h_bank1")
-        for s in range(2):
-            quantize_h(s * SLICE, SLICE)
-            second_layer(y_banks[s][:], s * SLICE, SLICE)
-        result_first = late.tile([P, SLICE], F32, name="result_first", align_bytes=ALIGN, offset=8192 + 2048)
-        nc.vector.tensor_copy(result_first[:], y_banks[0][:])
-        nc.sync.dma_start(out=out[:, part(0)], in_=result_first[:])
-        nc.scalar.copy(result[:, part(1)], y_banks[1][:])
-        nc.sync.dma_start(out=out[:, part(1)], in_=result[:, part(1)])
-        quantize_h(4 * GROUP, GROUP)
-        second_layer(y_late[:, :GROUP], 4 * GROUP, GROUP)
-        quantize_h(5 * GROUP, GROUP // 2)
-        second_layer(y_late[:, GROUP:], 5 * GROUP, GROUP // 2)
-        nc.scalar.copy(result[:, 4 * GROUP : last], y_late[:])
-        quantize_h(last, GROUP // 2)
-        second_layer(y_last[:], last, GROUP // 2)
-        nc.vector.tensor_copy(result[:, last:], y_last[:])
-        nc.sync.dma_start(out=out[:, part(2)], in_=result[:, part(2)])
+        result0 = reused.tile([P, SLICE], F32, name="result0", align_bytes=ALIGN, offset=h_offset + h_bytes)
+        nc.vector.tensor_copy(result0[:], y_banks[0][:])
+        nc.sync.dma_start(out=out[:, part(0)], in_=result0[:])
+        result1 = keep.tile([P, SLICE], F32, name="result1")
+        nc.scalar.copy(result1[:], y_banks[1][:])
+        nc.sync.dma_start(out=out[:, part(1)], in_=result1[:])
+
+        result2 = keep.tile([P, SLICE], F32, name="result2")
+        y_late = psum.tile([P, SLICE - HALF], F32, name="y_late", tag="h_bank0")
+        y_last = psum.tile([P, HALF], F32, name="y_last", tag="h_bank1")
+        second_product(y_late[:, :GROUP], 2 * SLICE, GROUP)
+        second_product(y_late[:, GROUP:], last - HALF, HALF)
+        nc.scalar.copy(result2[:, : SLICE - HALF], y_late[:])
+        second_product(y_last[:], last, HALF)
+        nc.vector.tensor_copy(result2[:, SLICE - HALF :], y_last[:])
+        nc.sync.dma_start(out=out[:, part(2)], in_=result2[:])

@@ -60,9 +60,11 @@ def tile_picked_pick_mlp_gelu_sub_e_kernel(tc, xT, w1, w2, offs, out):
                 nc.sync.dma_start(offsets[:], offs)
         w1_rows = w1.rearrange("(p j) h -> p j h", j=PACK)
         w1_pieces = []
-        for start, width in ((0, H // 2), (H // 2, H // 4), (3 * H // 4, H // 4)):
-            raw = keep.tile([P, PACK, width], F32, name=f"w1_raw{start}")
-            nc.sync.dma_start(out=raw[:], in_=w1_rows[:, :, start : start + width])
+        piece_places = (slice(0, PACK), slice(0, 2), slice(2, PACK))
+        for piece, places in enumerate(piece_places):
+            start = min(piece, 1) * (H // 2)
+            raw = keep.tile([P, places.stop - places.start, H // 2], F32, name=f"w1_raw{piece}")
+            nc.sync.dma_start(out=raw[:], in_=w1_rows[:, places, start : start + H // 2])
             w1_pieces.append(raw[:].rearrange("p j (a u b e) -> p u a j b e", u=2, b=2, e=2))
         w2_raw = keep.tile([P, PACK, N], F32, name="w2_raw")
         w2_rows = w2.rearrange("(a u b e) n -> b a u (e n)", u=2, b=2, e=2)
@@ -134,17 +136,16 @@ def tile_picked_pick_mlp_gelu_sub_e_kernel(tc, xT, w1, w2, offs, out):
         w1_shared = shared[:, : 2 * STAGED].rearrange("p (e c) -> p e c", e=2)
         w1_staged = [[w1_first[:, :2], w1_first[:, 2:]], [w1_last[:], w1_shared]]
 
-        def lay_out(copy, piece, half, rows, u):
-            to = w1_staged[half][u].rearrange("p e (a b j) -> p a j b e", b=2, j=PACK)
-            copy(to[:, rows], w1_pieces[piece][:, u])
+        def lay_out(copy, piece, u):
+            to = w1_staged[min(piece, 1)][u].rearrange("p e (a b j) -> p a j b e", b=2, j=PACK)
+            copy(to[:, :, piece_places[piece]], w1_pieces[piece][:, u])
 
-        quarter = HALF // 4
         for u in SIDES:
-            lay_out(nc.scalar.copy, 0, 0, slice(0, 2 * quarter), u)
+            lay_out(nc.scalar.copy, 0, u)
         for u in range(2):
-            lay_out(nc.vector.tensor_copy, 1, 1, slice(0, quarter), u)
-        lay_out(nc.scalar.copy, 2, 1, slice(quarter, 2 * quarter), 0)
-        lay_out(nc.vector.tensor_copy, 2, 1, slice(quarter, 2 * quarter), 1)
+            lay_out(nc.vector.tensor_copy, 1, u)
+        lay_out(nc.scalar.copy, 2, 0)
+        lay_out(nc.vector.tensor_copy, 2, 1)
         for half in range(2):
             for u in SIDES:
                 for e in range(2):

@@ -12,6 +12,7 @@ U16 = mybir.dt.uint16
 U8 = mybir.dt.uint8
 FP8X4 = mybir.dt.float8_e4m3fn_x4
 GELU = mybir.ActivationFunctionType.Gelu_apprx_tanh
+COPY = mybir.ActivationFunctionType.Copy
 
 P = 128
 PACK = 4
@@ -20,6 +21,7 @@ GROUP = 128
 HALF = 64
 ALIGN = 64
 SIDES = (1, 0)
+NEIGHBOURS = 8
 STAGED = HALF * PACK
 
 
@@ -60,10 +62,12 @@ def tile_picked_pick_mlp_gelu_sub_e_kernel(tc, xT, w1, w2, offs, out):
                 nc.sync.dma_start(offsets[:], offs)
         w1_rows = w1.rearrange("(p j) h -> p j h", j=PACK)
         w1_pieces = []
+        last_raw = 8192
         piece_places = (slice(0, PACK), slice(0, 2), slice(2, PACK))
         for piece, places in enumerate(piece_places):
             start = min(piece, 1) * (H // 2)
-            raw = keep.tile([P, places.stop - places.start, H // 2], F32, name=f"w1_raw{piece}")
+            shape = [P, places.stop - places.start, H // 2]
+            raw = reused.tile(shape, F32, name=f"w1_raw{piece}", align_bytes=ALIGN, offset=last_raw + (2 - piece) * 2048)
             nc.sync.dma_start(out=raw[:], in_=w1_rows[:, places, start : start + H // 2])
             w1_pieces.append(raw[:].rearrange("p j (a u b e) -> p u a j b e", u=2, b=2, e=2))
         w2_raw = keep.tile([P, PACK, N], F32, name="w2_raw")
@@ -76,94 +80,91 @@ def tile_picked_pick_mlp_gelu_sub_e_kernel(tc, xT, w1, w2, offs, out):
         table_out = keep.tile([P, 1], F32, name="table_out")
         nc.scalar.activation(table_out[:], table_in[:], GELU)
 
-        shared = keep.tile([P, STAGED + SLICE * PACK], BF16, name="shared", align_bytes=ALIGN)
-        x_flat = []
-        for s in range(slices - 1):
-            tile = keep.tile([P, SLICE * PACK], BF16, name=f"x_staged{s}", align_bytes=ALIGN)
-            x_flat.append(tile[:])
-        x_flat.append(shared[:, STAGED:])
-        x_staged = [flat.rearrange("p (n j) -> p n j", j=PACK) for flat in x_flat]
-
-        picked = keep.tile([P, 8, SLICE], F32, name="picked")
-        first_row = {2: 0, 0: 3, 1: 6}
-
-        def entries(s):
-            return offsets[:, s * (SLICE // 16) : (s + 1) * (SLICE // 16)]
+        late = S - SLICE
+        picked = keep.tile([P, 3 * SLICE + PACK * late + STAGED], BF16, name="picked", align_bytes=ALIGN)
+        early_rows = picked[:, : PACK * SLICE].rearrange("p (j n) -> p j n", j=PACK)
+        late_rows = picked[:, 3 * SLICE : 3 * SLICE + PACK * late].rearrange("p (j n) -> p j n", j=PACK)
+        x_first = keep.tile([P, SLICE, PACK], BF16, name="x_first", align_bytes=ALIGN)
 
         def part(s):
             return slice(s * SLICE, (s + 1) * SLICE)
 
-        def gather_into_place(j, s):
-            nc.vector.tensor_copy(x_staged[s][:, :, j], planes[j][:].indirect(entries(s)))
+        def looked_up(j, start, width):
+            return planes[j][:].indirect(offsets[:, start // 16 : (start + width) // 16])
 
-        def gather_plain(j, s):
-            nc.vector.tensor_copy(picked[:, first_row[s] + j, :], planes[j][:].indirect(entries(s)))
-
-        def interleave(s, places, tokens):
-            rows = slice(first_row[s] + places.start, first_row[s] + places.stop)
-            nc.scalar.copy(
-                x_staged[s][:, tokens, places].rearrange("p (c i) j -> p c j i", i=4),
-                picked[:, rows, tokens].rearrange("p j (c i) -> p c j i", i=4),
+        def interleave(copy, staged, rows):
+            copy(
+                staged.rearrange("p (c i) j -> p c j i", i=NEIGHBOURS),
+                rows.rearrange("p j (c i) -> p c j i", i=NEIGHBOURS),
             )
 
-        whole = slice(0, SLICE)
-        for j in range(2):
-            for s in range(slices):
-                gather_plain(j, s)
-        for s in range(2):
-            interleave(s, slice(0, 2), whole)
-        gather_plain(2, 0)
-        interleave(0, slice(2, PACK), whole)
-        gather_plain(2, 2)
-        interleave(2, slice(0, PACK), slice(HALF, SLICE))
-        gather_into_place(2, 1)
-        for s in range(2):
-            gather_into_place(3, s)
+        for j in range(3):
+            nc.vector.tensor_copy(early_rows[:, j, :], looked_up(j, 0, SLICE))
+            nc.vector.tensor_copy(late_rows[:, j, :SLICE], looked_up(j, SLICE, SLICE))
+            nc.scalar.activation(late_rows[:, j, SLICE:], looked_up(j, 2 * SLICE, SLICE), COPY)
+            if j == 1:
+                interleave(nc.scalar.copy, x_first[:, :, :2], early_rows[:, :2, :])
+        interleave(nc.scalar.copy, x_first[:, :, 2:], early_rows[:, 2:, :])
+        nc.vector.tensor_copy(x_first[:, :, 3], looked_up(3, 0, SLICE))
+        nc.scalar.activation(late_rows[:, 3, :SLICE], looked_up(3, SLICE, SLICE), COPY)
 
+        x_codes = keep.tile([P, S], U32, name="x_codes", align_bytes=ALIGN)
         x_scales = keep.tile([P, S], U8, name="x_scales", align_bytes=ALIGN)
-        x_codes = []
 
-        def quantize_x(codes, s):
-            quantize(nc, codes[:], x_scales[:, part(s)], x_flat[s])
-            x_codes.append(codes)
+        def quantize_x(staged, start, width):
+            cols = slice(start, start + width)
+            quantize(nc, x_codes[:, cols], x_scales[:, cols], staged[:].rearrange("p n j -> p (n j)"))
 
-        quantize_x(keep.tile([P, SLICE], U32, name="x_codes0", align_bytes=ALIGN), 0)
+        quantize_x(x_first, 0, SLICE)
 
         w1_codes = keep.tile([P, H], U32, name="w1_codes", align_bytes=ALIGN)
         w1_scales = keep.tile([P, H], U8, name="w1_scales", align_bytes=ALIGN)
         w1_first = keep.tile([P, PACK, STAGED], BF16, name="w1_first", align_bytes=ALIGN)
-        w1_last = reused.tile([P, 2, STAGED], BF16, name="w1_last", align_bytes=ALIGN, offset=512)
-        w1_shared = shared[:, : 2 * STAGED].rearrange("p (e c) -> p e c", e=2)
+        w1_last = reused.tile([P, 2, STAGED], BF16, name="w1_last", align_bytes=ALIGN, offset=0)
+        w1_shared = picked[:, 2 * SLICE + PACK * late :].rearrange("p (e c) -> p e c", e=2)
         w1_staged = [[w1_first[:, :2], w1_first[:, 2:]], [w1_last[:], w1_shared]]
 
-        def lay_out(copy, piece, u):
+        def lay_out(copy, piece, u, tiles):
             to = w1_staged[min(piece, 1)][u].rearrange("p e (a b j) -> p a j b e", b=2, j=PACK)
-            copy(to[:, :, piece_places[piece]], w1_pieces[piece][:, u])
+            copy(to[:, :, piece_places[piece], :, tiles], w1_pieces[piece][:, u, :, :, :, tiles])
 
-        for u in SIDES:
-            lay_out(nc.scalar.copy, 0, u)
-        for u in range(2):
-            lay_out(nc.vector.tensor_copy, 1, u)
-        lay_out(nc.scalar.copy, 2, 0)
-        lay_out(nc.vector.tensor_copy, 2, 1)
-        for half in range(2):
+        def quantize_w1(half):
             for u in SIDES:
                 for e in range(2):
                     start = (2 * u + e) * P + half * HALF
                     cols = slice(start, start + HALF)
                     quantize(nc, w1_codes[:, cols], w1_scales[:, cols], w1_staged[half][u][:, e, :])
 
-        quantize_x(reused.tile([P, SLICE], U32, name="x_codes1", align_bytes=ALIGN, offset=0), 1)
-        interleave(2, slice(0, PACK), slice(0, HALF))
-        gather_into_place(3, 2)
-        w2_staged = reused.tile([P, N, PACK], BF16, name="w2_staged", align_bytes=ALIGN, offset=1024)
+        for piece in range(2):
+            lay_out(nc.vector.tensor_copy, piece, 1, slice(0, 2))
+            lay_out(nc.scalar.copy, piece, 0, slice(0, 2))
+        lay_out(nc.scalar.copy, 2, 0, slice(0, 1))
+        for u, e in ((1, 0), (1, 1), (0, 1)):
+            lay_out(nc.vector.tensor_copy, 2, u, slice(e, e + 1))
+        for half in range(2):
+            quantize_w1(half)
+
+        def stage_x(copy, g, offset):
+            tile = reused.tile([P, GROUP, PACK], BF16, name=f"x_staged{g}", align_bytes=ALIGN, offset=offset)
+            start = g * GROUP - SLICE
+            interleave(copy, tile[:], late_rows[:, :, start : start + GROUP])
+            return tile
+
+        nc.scalar.activation(late_rows[:, 3, SLICE:], looked_up(3, 2 * SLICE, SLICE), COPY)
+        ring = (last_raw, last_raw + GROUP * PACK * 2)
+        staged = [stage_x(nc.vector.tensor_copy, 2 + k, ring[k]) for k in range(2)]
+        for k in range(2):
+            quantize_x(staged[k], (2 + k) * GROUP, GROUP)
+        w2_staged = reused.tile([P, N, PACK], BF16, name="w2_staged", align_bytes=ALIGN, offset=0)
         nc.vector.tensor_copy(
             w2_staged[:].rearrange("p (c i) t -> p c t i", i=4), w2_raw[:].rearrange("p t (c i) -> p c t i", i=4)
         )
-        quantize_x(keep.tile([P, SLICE], U32, name="x_codes2", align_bytes=ALIGN), 2)
+        staged = [stage_x(nc.vector.tensor_copy, 4 + k, ring[k]) for k in range(2)]
+        quantize_x(staged[0], 4 * GROUP, GROUP)
         w2_codes = keep.tile([P, N], U32, name="w2_codes", align_bytes=ALIGN)
         w2_scales = keep.tile([P, N], U8, name="w2_scales", align_bytes=ALIGN)
         quantize(nc, w2_codes[:], w2_scales[:], w2_staged[:].rearrange("p n t -> p (n t)"))
+        quantize_x(staged[1], 5 * GROUP, GROUP)
 
         h_offset, h_bytes = 2048, SLICE * PACK * 2
         h_staged = []
@@ -188,7 +189,7 @@ def tile_picked_pick_mlp_gelu_sub_e_kernel(tc, xT, w1, w2, offs, out):
         last = S - HALF
         for g in range(groups):
             start = g * GROUP
-            tokens = x_codes[start // SLICE][:, start % SLICE : start % SLICE + GROUP]
+            tokens = x_codes[:, start : start + GROUP]
             for u in SIDES:
                 for t in (2 * u, 2 * u + 1):
                     cols = slice(t * P, (t + 1) * P)

@@ -22,6 +22,7 @@ HALF = 64
 ALIGN = 64
 SIDES = (1, 0)
 NEIGHBOURS = 8
+WARM_M, WARM_N = 32, 512
 STAGED = HALF * PACK
 
 
@@ -107,6 +108,17 @@ def tile_picked_pick_mlp_gelu_sub_e_kernel(tc, xT, w1, w2, offs, out):
         interleave(nc.scalar.copy, x_first[:, :, 2:], early_rows[:, 2:, :])
         nc.vector.tensor_copy(x_first[:, :, 3], looked_up(3, 0, SLICE))
         nc.scalar.activation(late_rows[:, 3, :SLICE], looked_up(3, SLICE, SLICE), COPY)
+
+        warm_codes = keep.tile([P, WARM_N + WARM_M], U32, name="warm_codes", align_bytes=ALIGN)
+        warm_scales = keep.tile([P, WARM_N + HALF], U8, name="warm_scales", align_bytes=ALIGN)
+        moving = slice(0, WARM_N)
+        quantize(nc, warm_codes[:, moving], warm_scales[:, moving], picked[:, : WARM_N * PACK])
+        second = slice(WARM_N, WARM_N + WARM_M)
+        quantize(nc, warm_codes[:, second], warm_scales[:, second], late_rows[:, 3, : WARM_M * PACK])
+        warm_bank = psum.tile([WARM_M, WARM_N], F32, name="warm_bank", tag="y_bank1")
+        for still in (slice(0, WARM_M), second, second):
+            stationary = (warm_codes[:, still], warm_scales[:, still])
+            multiply(nc, warm_bank[:], *stationary, warm_codes[:, moving], warm_scales[:, moving])
 
         x_codes = keep.tile([P, S], U32, name="x_codes", align_bytes=ALIGN)
         x_scales = keep.tile([P, S], U8, name="x_scales", align_bytes=ALIGN)

@@ -116,7 +116,7 @@ def tile_picked_pick_mlp_gelu_sub_e_kernel(tc, xT, w1, w2, offs, out):
         second = slice(WARM_N, WARM_N + WARM_M)
         quantize(nc, warm_codes[:, second], warm_scales[:, second], late_rows[:, 3, : WARM_M * PACK])
         warm_bank = psum.tile([WARM_M, WARM_N], F32, name="warm_bank", tag="y_bank1")
-        for still in (slice(0, WARM_M), second, second):
+        for still in (second, second, second):
             stationary = (warm_codes[:, still], warm_scales[:, still])
             multiply(nc, warm_bank[:], *stationary, warm_codes[:, moving], warm_scales[:, moving])
 

@@ -107,14 +107,15 @@ def tile_picked_pick_mlp_gelu_sub_e_kernel(tc, xT, w1, w2, offs, out):
                 interleave(nc.scalar.copy, x_first[:, :, :2], early_rows[:, :2, :])
         interleave(nc.scalar.copy, x_first[:, :, 2:], early_rows[:, 2:, :])
         nc.vector.tensor_copy(x_first[:, :, 3], looked_up(3, 0, SLICE))
-        nc.scalar.activation(late_rows[:, 3, :SLICE], looked_up(3, SLICE, SLICE), COPY)
+        nc.scalar.activation(late_rows[:, 3, :HALF], looked_up(3, SLICE, HALF), COPY)
+        nc.scalar.activation(late_rows[:, 3, HALF:SLICE], looked_up(3, SLICE + HALF, SLICE - HALF), COPY)
 
         warm_codes = keep.tile([P, WARM_N + WARM_M], U32, name="warm_codes", align_bytes=ALIGN)
         warm_scales = keep.tile([P, WARM_N + HALF], U8, name="warm_scales", align_bytes=ALIGN)
         moving = slice(0, WARM_N)
         quantize(nc, warm_codes[:, moving], warm_scales[:, moving], picked[:, : WARM_N * PACK])
         second = slice(WARM_N, WARM_N + WARM_M)
-        quantize(nc, warm_codes[:, second], warm_scales[:, second], late_rows[:, 3, : WARM_M * PACK])
+        quantize(nc, warm_codes[:, second], warm_scales[:, second], picked[:, 3 * S - HALF : 3 * S + HALF])
         warm_bank = psum.tile([WARM_M, WARM_N], F32, name="warm_bank", tag="y_bank1")
         for still in (second, second, second):
             stationary = (warm_codes[:, still], warm_scales[:, still])

@@ -21,7 +21,7 @@ GROUP = 128
 HALF = 64
 ALIGN = 64
 SIDES = (1, 0)
-NEIGHBOURS = 8
+NEIGHBOURS = 4
 WARM_M, WARM_N = 32, 512
 STAGED = HALF * PACK
 
@@ -82,9 +82,10 @@ def tile_picked_pick_mlp_gelu_sub_e_kernel(tc, xT, w1, w2, offs, out):
         nc.scalar.activation(table_out[:], table_in[:], GELU)
 
         late = S - SLICE
-        picked = keep.tile([P, 3 * SLICE + PACK * late + STAGED], BF16, name="picked", align_bytes=ALIGN)
-        early_rows = picked[:, : PACK * SLICE].rearrange("p (j n) -> p j n", j=PACK)
-        late_rows = picked[:, 3 * SLICE : 3 * SLICE + PACK * late].rearrange("p (j n) -> p j n", j=PACK)
+        picked = keep.tile([P, 2 * SLICE + PACK * late + STAGED], BF16, name="picked", align_bytes=ALIGN)
+        early_low = picked[:, : 2 * SLICE].rearrange("p (j n) -> p j n", j=2)
+        early_high = keep.tile([P, 2, SLICE], BF16, name="early_high", align_bytes=ALIGN)
+        late_rows = picked[:, 2 * SLICE : 2 * SLICE + PACK * late].rearrange("p (j n) -> p j n", j=PACK)
         x_first = keep.tile([P, SLICE, PACK], BF16, name="x_first", align_bytes=ALIGN)
 
         def part(s):
@@ -100,41 +101,45 @@ def tile_picked_pick_mlp_gelu_sub_e_kernel(tc, xT, w1, w2, offs, out):
             )
 
         for j in range(3):
-            nc.vector.tensor_copy(early_rows[:, j, :], looked_up(j, 0, SLICE))
+            nc.vector.tensor_copy((early_low, early_high)[j // 2][:, j % 2, :], looked_up(j, 0, SLICE))
             nc.vector.tensor_copy(late_rows[:, j, :SLICE], looked_up(j, SLICE, SLICE))
             nc.scalar.activation(late_rows[:, j, SLICE:], looked_up(j, 2 * SLICE, SLICE), COPY)
             if j == 1:
-                interleave(nc.scalar.copy, x_first[:, :, :2], early_rows[:, :2, :])
-        interleave(nc.scalar.copy, x_first[:, :, 2:], early_rows[:, 2:, :])
-        nc.vector.tensor_copy(x_first[:, :, 3], looked_up(3, 0, SLICE))
-        nc.scalar.activation(late_rows[:, 3, :HALF], looked_up(3, SLICE, HALF), COPY)
-        nc.scalar.activation(late_rows[:, 3, HALF:SLICE], looked_up(3, SLICE + HALF, SLICE - HALF), COPY)
+                interleave(nc.scalar.copy, x_first[:, :, :2], early_low)
+        halves = (slice(0, GROUP), slice(GROUP, SLICE))
+        for half in halves:
+            nc.vector.tensor_copy(early_high[:, 1, half], looked_up(3, half.start, GROUP))
 
         warm_codes = keep.tile([P, WARM_N + WARM_M], U32, name="warm_codes", align_bytes=ALIGN)
         warm_scales = keep.tile([P, WARM_N + HALF], U8, name="warm_scales", align_bytes=ALIGN)
         moving = slice(0, WARM_N)
         quantize(nc, warm_codes[:, moving], warm_scales[:, moving], picked[:, : WARM_N * PACK])
         second = slice(WARM_N, WARM_N + WARM_M)
-        quantize(nc, warm_codes[:, second], warm_scales[:, second], picked[:, 3 * S - HALF : 3 * S + HALF])
+        quantize(nc, warm_codes[:, second], warm_scales[:, second], early_high[:].rearrange("p j n -> p (j n)")[:, SLICE - HALF : SLICE + HALF])
         warm_bank = psum.tile([WARM_M, WARM_N], F32, name="warm_bank", tag="y_bank1")
         for still in (second, second, second):
             stationary = (warm_codes[:, still], warm_scales[:, still])
             multiply(nc, warm_bank[:], *stationary, warm_codes[:, moving], warm_scales[:, moving])
+
+        for half in halves:
+            interleave(nc.vector.tensor_copy, x_first[:, half, 2:], early_high[:, :, half])
+        nc.scalar.activation(late_rows[:, 3, :SLICE], looked_up(3, SLICE, SLICE), COPY)
 
         x_codes = keep.tile([P, S], U32, name="x_codes", align_bytes=ALIGN)
         x_scales = keep.tile([P, S], U8, name="x_scales", align_bytes=ALIGN)
 
         def quantize_x(staged, start, width):
             cols = slice(start, start + width)
-            quantize(nc, x_codes[:, cols], x_scales[:, cols], staged[:].rearrange("p n j -> p (n j)"))
+            quantize(nc, x_codes[:, cols], x_scales[:, cols], staged.rearrange("p n j -> p (n j)"))
 
-        quantize_x(x_first, 0, SLICE)
+        for half in halves:
+            quantize_x(x_first[:, half], half.start, GROUP)
 
         w1_codes = keep.tile([P, H], U32, name="w1_codes", align_bytes=ALIGN)
         w1_scales = keep.tile([P, H], U8, name="w1_scales", align_bytes=ALIGN)
         w1_first = keep.tile([P, PACK, STAGED], BF16, name="w1_first", align_bytes=ALIGN)
         w1_last = reused.tile([P, 2, STAGED], BF16, name="w1_last", align_bytes=ALIGN, offset=0)
-        w1_shared = picked[:, 2 * SLICE + PACK * late :].rearrange("p (e c) -> p e c", e=2)
+        w1_shared = picked[:, SLICE + PACK * late :].rearrange("p (e c) -> p e c", e=2)
         w1_staged = [[w1_first[:, :2], w1_first[:, 2:]], [w1_last[:], w1_shared]]
 
         def lay_out(copy, piece, u, tiles):
@@ -167,17 +172,17 @@ def tile_picked_pick_mlp_gelu_sub_e_kernel(tc, xT, w1, w2, offs, out):
         ring = (last_raw, last_raw + GROUP * PACK * 2)
         staged = [stage_x(nc.vector.tensor_copy, 2 + k, ring[k]) for k in range(2)]
         for k in range(2):
-            quantize_x(staged[k], (2 + k) * GROUP, GROUP)
+            quantize_x(staged[k][:], (2 + k) * GROUP, GROUP)
         w2_staged = reused.tile([P, N, PACK], BF16, name="w2_staged", align_bytes=ALIGN, offset=0)
         nc.vector.tensor_copy(
             w2_staged[:].rearrange("p (c i) t -> p c t i", i=4), w2_raw[:].rearrange("p t (c i) -> p c t i", i=4)
         )
         staged = [stage_x(nc.vector.tensor_copy, 4 + k, ring[k]) for k in range(2)]
-        quantize_x(staged[0], 4 * GROUP, GROUP)
+        quantize_x(staged[0][:], 4 * GROUP, GROUP)
         w2_codes = keep.tile([P, N], U32, name="w2_codes", align_bytes=ALIGN)
         w2_scales = keep.tile([P, N], U8, name="w2_scales", align_bytes=ALIGN)
         quantize(nc, w2_codes[:], w2_scales[:], w2_staged[:].rearrange("p n t -> p (n t)"))
-        quantize_x(staged[1], 5 * GROUP, GROUP)
+        quantize_x(staged[1][:], 5 * GROUP, GROUP)
 
         h_offset, h_bytes = 2048, SLICE * PACK * 2
         h_staged = []

@@ -132,8 +132,7 @@ def tile_picked_pick_mlp_gelu_sub_e_kernel(tc, xT, w1, w2, offs, out):
             cols = slice(start, start + width)
             quantize(nc, x_codes[:, cols], x_scales[:, cols], staged.rearrange("p n j -> p (n j)"))
 
-        for half in halves:
-            quantize_x(x_first[:, half], half.start, GROUP)
+        quantize_x(x_first[:, :GROUP], 0, GROUP)
 
         w1_codes = keep.tile([P, H], U32, name="w1_codes", align_bytes=ALIGN)
         w1_scales = keep.tile([P, H], U8, name="w1_scales", align_bytes=ALIGN)
@@ -168,9 +167,11 @@ def tile_picked_pick_mlp_gelu_sub_e_kernel(tc, xT, w1, w2, offs, out):
             interleave(copy, tile[:], late_rows[:, :, start : start + GROUP])
             return tile
 
+        codes1 = reused.tile([P, GROUP], U32, name="codes1", align_bytes=ALIGN, offset=last_raw - 256)
+        quantize(nc, codes1[:], x_scales[:, GROUP:SLICE], x_first[:, GROUP:].rearrange("p n j -> p (n j)"))
+        ring = (last_raw + 256, last_raw + 256 + GROUP * PACK * 2)
+        staged = [stage_x(nc.vector.tensor_copy, 2, ring[0]), stage_x(nc.vector.tensor_copy, 3, ring[1])]
         nc.scalar.activation(late_rows[:, 3, SLICE:], looked_up(3, 2 * SLICE, SLICE), COPY)
-        ring = (last_raw, last_raw + GROUP * PACK * 2)
-        staged = [stage_x(nc.vector.tensor_copy, 2 + k, ring[k]) for k in range(2)]
         for k in range(2):
             quantize_x(staged[k][:], (2 + k) * GROUP, GROUP)
         w2_staged = reused.tile([P, N, PACK], BF16, name="w2_staged", align_bytes=ALIGN, offset=0)
@@ -207,7 +208,7 @@ def tile_picked_pick_mlp_gelu_sub_e_kernel(tc, xT, w1, w2, offs, out):
         last = S - HALF
         for g in range(groups):
             start = g * GROUP
-            tokens = x_codes[:, start : start + GROUP]
+            tokens = codes1[:] if g == 1 else x_codes[:, start : start + GROUP]
             for u in SIDES:
                 for t in (2 * u, 2 * u + 1):
                     cols = slice(t * P, (t + 1) * P)

@@ -53,28 +53,18 @@ def tile_picked_pick_mlp_gelu_sub_e_kernel(tc, xT, w1, w2, offs, out):
         psum = ctx.enter_context(tc.psum_pool(name="psum", bufs=1))
 
         offsets = keep.tile([P, S // 16], U16, name="offsets")
+        nc.sync.dma_start(offsets[:], offs)
         planes = []
+        last_raw = 8192
         x_rows = xT.rearrange("(p j) t -> p j t", j=PACK)
         for j in range(PACK):
-            plane = keep.tile([P, T], F32, name=f"plane{j}")
-            nc.sync.dma_start(out=plane[:], in_=x_rows[:, j, :])
+            if j == 1:
+                plane = reused.tile([P, T], F32, name="plane1", align_bytes=ALIGN, offset=last_raw)
+            else:
+                plane = keep.tile([P, T], F32, name=f"plane{j}")
+            queue = nc.scalar if j == 0 else nc.sync
+            queue.dma_start(out=plane[:], in_=x_rows[:, j, :])
             planes.append(plane)
-            if j == 0:
-                nc.sync.dma_start(offsets[:], offs)
-        w1_rows = w1.rearrange("(p j) h -> p j h", j=PACK)
-        w1_pieces = []
-        last_raw = 8192
-        piece_places = (slice(0, PACK), slice(0, 2), slice(2, PACK))
-        for piece, places in enumerate(piece_places):
-            start = min(piece, 1) * (H // 2)
-            shape = [P, places.stop - places.start, H // 2]
-            raw = reused.tile(shape, F32, name=f"w1_raw{piece}", align_bytes=ALIGN, offset=last_raw + (2 - piece) * 2048)
-            nc.sync.dma_start(out=raw[:], in_=w1_rows[:, places, start : start + H // 2])
-            w1_pieces.append(raw[:].rearrange("p j (a u b e) -> p u a j b e", u=2, b=2, e=2))
-        w2_raw = keep.tile([P, PACK, N], F32, name="w2_raw")
-        w2_rows = w2.rearrange("(a u b e) n -> b a u (e n)", u=2, b=2, e=2)
-        for b in range(2):
-            nc.sync.dma_start(out=w2_raw[b::2].rearrange("p (u e) n -> p u (e n)", u=2), in_=w2_rows[b])
 
         table_in = keep.tile([P, 1], F32, name="table_in")
         nc.vector.memset(table_in[:], 0.0)
@@ -84,7 +74,7 @@ def tile_picked_pick_mlp_gelu_sub_e_kernel(tc, xT, w1, w2, offs, out):
         late = S - SLICE
         picked = keep.tile([P, 2 * SLICE + PACK * late + STAGED], BF16, name="picked", align_bytes=ALIGN)
         early_low = picked[:, : 2 * SLICE].rearrange("p (j n) -> p j n", j=2)
-        early_high = keep.tile([P, 2, SLICE], BF16, name="early_high", align_bytes=ALIGN)
+        early_high = reused.tile([P, 2, SLICE], BF16, name="early_high", align_bytes=ALIGN, offset=20480)
         late_rows = picked[:, 2 * SLICE : 2 * SLICE + PACK * late].rearrange("p (j n) -> p j n", j=PACK)
         x_first = keep.tile([P, SLICE, PACK], BF16, name="x_first", align_bytes=ALIGN)
 
@@ -106,6 +96,19 @@ def tile_picked_pick_mlp_gelu_sub_e_kernel(tc, xT, w1, w2, offs, out):
             nc.scalar.activation(late_rows[:, j, SLICE:], looked_up(j, 2 * SLICE, SLICE), COPY)
             if j == 1:
                 interleave(nc.scalar.copy, x_first[:, :, :2], early_low)
+
+        w1_rows = w1.rearrange("(p j) h -> p j h", j=PACK)
+        w1_pieces = []
+        piece_places = (slice(0, PACK), slice(0, 2), slice(2, PACK))
+        for piece, places in enumerate(piece_places):
+            start = min(piece, 1) * (H // 2)
+            shape = [P, places.stop - places.start, H // 2]
+            raw = reused.tile(shape, F32, name=f"w1_raw{piece}", align_bytes=ALIGN, offset=last_raw + (2 - piece) * 2048)
+            rows = w1_rows[:, places, start : start + H // 2]
+            middle = shape[1] // 2
+            nc.sync.dma_start(out=raw[:, :middle], in_=rows[:, :middle])
+            nc.scalar.dma_start(out=raw[:, middle:], in_=rows[:, middle:])
+            w1_pieces.append(raw[:].rearrange("p j (a u b e) -> p u a j b e", u=2, b=2, e=2))
         halves = (slice(0, GROUP), slice(GROUP, SLICE))
         for half in halves:
             nc.vector.tensor_copy(early_high[:, 1, half], looked_up(3, half.start, GROUP))
@@ -124,6 +127,11 @@ def tile_picked_pick_mlp_gelu_sub_e_kernel(tc, xT, w1, w2, offs, out):
         for half in halves:
             interleave(nc.vector.tensor_copy, x_first[:, half, 2:], early_high[:, :, half])
         nc.scalar.activation(late_rows[:, 3, :SLICE], looked_up(3, SLICE, SLICE), COPY)
+        w2_raw = reused.tile([P, PACK, N], F32, name="w2_raw", align_bytes=ALIGN, offset=20480)
+        w2_rows = w2.rearrange("(a u b e) n -> b a u (e n)", u=2, b=2, e=2)
+        for b in range(2):
+            nc.sync.dma_start(out=w2_raw[b::2].rearrange("p (u e) n -> p u (e n)", u=2), in_=w2_rows[b])
+
 
         x_codes = keep.tile([P, S], U32, name="x_codes", align_bytes=ALIGN)
         x_scales = keep.tile([P, S], U8, name="x_scales", align_bytes=ALIGN)

@@ -20,10 +20,9 @@ SLICE = 256
 GROUP = 128
 HALF = 64
 ALIGN = 64
-SIDES = (1, 0)
 NEIGHBOURS = 4
 WARM_M, WARM_N = 32, 512
-STAGED = HALF * PACK
+STAGED_BYTES = GROUP * PACK * 2
 
 
 def quantize(nc, codes, scales, values):
@@ -42,217 +41,176 @@ def multiply(nc, product, weights, weight_scales, tokens, token_scales):
     )
 
 
+def interleave(copy, staged, rows):
+    copy(
+        staged.rearrange("p (c i) j -> p c j i", i=NEIGHBOURS),
+        rows.rearrange("p j (c i) -> p c j i", i=NEIGHBOURS),
+    )
+
+
+def flat(staged):
+    return staged.rearrange("p n j -> p (n j)")
+
+
 def tile_picked_pick_mlp_gelu_sub_e_kernel(tc, xT, w1, w2, offs, out):
     nc = tc.nc
-    slices = S // SLICE
     groups = S // GROUP
 
     with ExitStack() as ctx:
         keep = ctx.enter_context(tc.tile_pool(name="keep", bufs=1))
-        reused = ctx.enter_context(tc.tile_pool(name="reused", bufs=1))
+        placed = ctx.enter_context(tc.tile_pool(name="placed", bufs=1))
         psum = ctx.enter_context(tc.psum_pool(name="psum", bufs=1))
 
         offsets = keep.tile([P, S // 16], U16, name="offsets")
-        nc.sync.dma_start(offsets[:], offs)
-        planes = []
-        last_raw = 8192
         x_rows = xT.rearrange("(p j) t -> p j t", j=PACK)
-        for j in range(PACK):
-            if j == 1:
-                plane = reused.tile([P, T], F32, name="plane1", align_bytes=ALIGN, offset=last_raw)
-            else:
-                plane = keep.tile([P, T], F32, name=f"plane{j}")
-            queue = nc.scalar if j == 0 else nc.sync
-            queue.dma_start(out=plane[:], in_=x_rows[:, j, :])
-            planes.append(plane)
+        planes = [keep.tile([P, T], F32, name=f"plane{j}") for j in range(PACK)]
+        nc.sync.dma_start(out=planes[0][:], in_=x_rows[:, 0, :])
+        nc.scalar.dma_start(out=planes[1][:], in_=x_rows[:, 1, :])
+        nc.sync.dma_start(offsets[:], offs)
+        for j in range(2, PACK):
+            nc.sync.dma_start(out=planes[j][:], in_=x_rows[:, j, :])
+        raw_offset = PACK * STAGED_BYTES
+        w1_raw = placed.tile([P, PACK, H], F32, name="w1_raw", align_bytes=ALIGN, offset=raw_offset)
+        nc.sync.dma_start(out=w1_raw[:], in_=w1.rearrange("(p j) h -> p j h", j=PACK))
+        w2_raw = keep.tile([P, PACK, N], F32, name="w2_raw")
+        w2_rows = w2.rearrange("(a t r) n -> r a t n", t=PACK, r=NEIGHBOURS)
+        for r in range(NEIGHBOURS):
+            nc.sync.dma_start(out=w2_raw[r::NEIGHBOURS], in_=w2_rows[r])
 
         table_in = keep.tile([P, 1], F32, name="table_in")
         nc.vector.memset(table_in[:], 0.0)
         table_out = keep.tile([P, 1], F32, name="table_out")
         nc.scalar.activation(table_out[:], table_in[:], GELU)
 
-        late = S - SLICE
-        picked = keep.tile([P, 2 * SLICE + PACK * late + STAGED], BF16, name="picked", align_bytes=ALIGN)
-        early_low = picked[:, : 2 * SLICE].rearrange("p (j n) -> p j n", j=2)
-        early_high = reused.tile([P, 2, SLICE], BF16, name="early_high", align_bytes=ALIGN, offset=20480)
-        late_rows = picked[:, 2 * SLICE : 2 * SLICE + PACK * late].rearrange("p (j n) -> p j n", j=PACK)
-        x_first = keep.tile([P, SLICE, PACK], BF16, name="x_first", align_bytes=ALIGN)
+        picked = keep.tile([P, PACK, S], BF16, name="picked", align_bytes=ALIGN)
 
-        def part(s):
-            return slice(s * SLICE, (s + 1) * SLICE)
+        def gather(engine_copy, j, start, width):
+            window = planes[j][:].indirect(offsets[:, start // 16 : (start + width) // 16])
+            engine_copy(picked[:, j, start : start + width], window)
 
-        def looked_up(j, start, width):
-            return planes[j][:].indirect(offsets[:, start // 16 : (start + width) // 16])
+        def scalar_gather(to, window):
+            nc.scalar.activation(to, window, COPY)
 
-        def interleave(copy, staged, rows):
-            copy(
-                staged.rearrange("p (c i) j -> p c j i", i=NEIGHBOURS),
-                rows.rearrange("p j (c i) -> p c j i", i=NEIGHBOURS),
-            )
-
-        for j in range(3):
-            nc.vector.tensor_copy((early_low, early_high)[j // 2][:, j % 2, :], looked_up(j, 0, SLICE))
-            nc.vector.tensor_copy(late_rows[:, j, :SLICE], looked_up(j, SLICE, SLICE))
-            nc.scalar.activation(late_rows[:, j, SLICE:], looked_up(j, 2 * SLICE, SLICE), COPY)
-            if j == 1:
-                interleave(nc.scalar.copy, x_first[:, :, :2], early_low)
-
-        w1_rows = w1.rearrange("(p j) h -> p j h", j=PACK)
-        w1_pieces = []
-        piece_places = (slice(0, PACK), slice(0, 2), slice(2, PACK))
-        for piece, places in enumerate(piece_places):
-            start = min(piece, 1) * (H // 2)
-            shape = [P, places.stop - places.start, H // 2]
-            raw = reused.tile(shape, F32, name=f"w1_raw{piece}", align_bytes=ALIGN, offset=last_raw + (2 - piece) * 2048)
-            rows = w1_rows[:, places, start : start + H // 2]
-            middle = shape[1] // 2
-            nc.sync.dma_start(out=raw[:, :middle], in_=rows[:, :middle])
-            nc.scalar.dma_start(out=raw[:, middle:], in_=rows[:, middle:])
-            w1_pieces.append(raw[:].rearrange("p j (a u b e) -> p u a j b e", u=2, b=2, e=2))
-        halves = (slice(0, GROUP), slice(GROUP, SLICE))
-        for half in halves:
-            nc.vector.tensor_copy(early_high[:, 1, half], looked_up(3, half.start, GROUP))
+        for j in range(PACK - 1):
+            gather(nc.vector.tensor_copy, j, 0, S // 2)
+            gather(scalar_gather, j, S // 2, S // 2)
 
         warm_codes = keep.tile([P, WARM_N + WARM_M], U32, name="warm_codes", align_bytes=ALIGN)
         warm_scales = keep.tile([P, WARM_N + HALF], U8, name="warm_scales", align_bytes=ALIGN)
         moving = slice(0, WARM_N)
-        quantize(nc, warm_codes[:, moving], warm_scales[:, moving], picked[:, : WARM_N * PACK])
-        second = slice(WARM_N, WARM_N + WARM_M)
-        quantize(nc, warm_codes[:, second], warm_scales[:, second], early_high[:].rearrange("p j n -> p (j n)")[:, SLICE - HALF : SLICE + HALF])
-        warm_bank = psum.tile([WARM_M, WARM_N], F32, name="warm_bank", tag="y_bank1")
-        for still in (second, second, second):
+        still = slice(WARM_N, WARM_N + WARM_M)
+        picked_rows = picked[:].rearrange("p j n -> p (j n)")
+        quantize(nc, warm_codes[:, moving], warm_scales[:, moving], picked_rows[:, : WARM_N * PACK])
+
+        for g in range(2):
+            gather(nc.vector.tensor_copy, 3, g * GROUP, GROUP)
+        for s in range(1, 3):
+            gather(scalar_gather, 3, s * SLICE, SLICE)
+
+        quantize(nc, warm_codes[:, still], warm_scales[:, still], picked[:, 3, : WARM_M * PACK])
+        warm_bank = psum.tile([WARM_M, WARM_N], F32, name="warm_bank", tag="h_bank5")
+        for turn in range(3):
             stationary = (warm_codes[:, still], warm_scales[:, still])
             multiply(nc, warm_bank[:], *stationary, warm_codes[:, moving], warm_scales[:, moving])
 
-        for half in halves:
-            interleave(nc.vector.tensor_copy, x_first[:, half, 2:], early_high[:, :, half])
-        nc.scalar.activation(late_rows[:, 3, :SLICE], looked_up(3, SLICE, SLICE), COPY)
-        w2_raw = reused.tile([P, PACK, N], F32, name="w2_raw", align_bytes=ALIGN, offset=20480)
-        w2_rows = w2.rearrange("(a u b e) n -> b a u (e n)", u=2, b=2, e=2)
-        for b in range(2):
-            nc.sync.dma_start(out=w2_raw[b::2].rearrange("p (u e) n -> p u (e n)", u=2), in_=w2_rows[b])
+        def stage_x(copy, g, pool, **place):
+            tile = pool.tile([P, GROUP, PACK], BF16, name=f"x_staged{g}", align_bytes=ALIGN, **place)
+            interleave(copy, tile[:], picked[:, :, g * GROUP : (g + 1) * GROUP])
+            return tile
 
-
-        x_codes = keep.tile([P, S], U32, name="x_codes", align_bytes=ALIGN)
         x_scales = keep.tile([P, S], U8, name="x_scales", align_bytes=ALIGN)
+        head_codes = keep.tile([P, SLICE], U32, name="head_codes", align_bytes=ALIGN)
 
-        def quantize_x(staged, start, width):
-            cols = slice(start, start + width)
-            quantize(nc, x_codes[:, cols], x_scales[:, cols], staged.rearrange("p n j -> p (n j)"))
+        def quantize_x(codes, g):
+            quantize(nc, codes, x_scales[:, g * GROUP : (g + 1) * GROUP], flat(staged[g][:]))
 
-        quantize_x(x_first[:, :GROUP], 0, GROUP)
+        staged = [stage_x(nc.vector.tensor_copy, g, keep) for g in range(2)]
+        quantize_x(head_codes[:, :GROUP], 0)
+        staged.append(stage_x(nc.vector.tensor_copy, 2, keep))
+        quantize_x(head_codes[:, GROUP:], 1)
+        staged.append(stage_x(nc.scalar.copy, 3, keep))
 
         w1_codes = keep.tile([P, H], U32, name="w1_codes", align_bytes=ALIGN)
         w1_scales = keep.tile([P, H], U8, name="w1_scales", align_bytes=ALIGN)
-        w1_first = keep.tile([P, PACK, STAGED], BF16, name="w1_first", align_bytes=ALIGN)
-        w1_last = reused.tile([P, 2, STAGED], BF16, name="w1_last", align_bytes=ALIGN, offset=0)
-        w1_shared = picked[:, SLICE + PACK * late :].rearrange("p (e c) -> p e c", e=2)
-        w1_staged = [[w1_first[:, :2], w1_first[:, 2:]], [w1_last[:], w1_shared]]
+        w1_tiles = w1_raw[:].rearrange("p j (a t r) -> p t a j r", t=PACK, r=NEIGHBOURS)
+        w1_staged = []
+        for t, copy in enumerate((nc.vector.tensor_copy, nc.scalar.copy, nc.vector.tensor_copy, nc.scalar.copy)):
+            tile = placed.tile([P, P, PACK], BF16, name=f"w1_staged{t}", align_bytes=ALIGN, offset=t * STAGED_BYTES)
+            copy(tile[:].rearrange("p (a r) j -> p a j r", r=NEIGHBOURS), w1_tiles[:, t])
+            w1_staged.append(tile)
 
-        def lay_out(copy, piece, u, tiles):
-            to = w1_staged[min(piece, 1)][u].rearrange("p e (a b j) -> p a j b e", b=2, j=PACK)
-            copy(to[:, :, piece_places[piece], :, tiles], w1_pieces[piece][:, u, :, :, :, tiles])
+        def w1_tile(t):
+            return w1_codes[:, t * P : (t + 1) * P], w1_scales[:, t * P : (t + 1) * P]
 
-        def quantize_w1(half):
-            for u in SIDES:
-                for e in range(2):
-                    start = (2 * u + e) * P + half * HALF
-                    cols = slice(start, start + HALF)
-                    quantize(nc, w1_codes[:, cols], w1_scales[:, cols], w1_staged[half][u][:, e, :])
+        h_rows = keep.tile([P, PACK, SLICE], BF16, name="h_rows", align_bytes=ALIGN)
+        for t in range(PACK):
+            quantize(nc, *w1_tile(t), flat(w1_staged[t][:]))
+            bank = psum.tile([P, SLICE], F32, name=f"head_bank{t}")
+            multiply(nc, bank[:], *w1_tile(t), head_codes[:], x_scales[:, :SLICE])
+            nc.scalar.activation(h_rows[:, t, :], bank[:], GELU)
 
-        for piece in range(2):
-            lay_out(nc.vector.tensor_copy, piece, 1, slice(0, 2))
-            lay_out(nc.scalar.copy, piece, 0, slice(0, 2))
-        lay_out(nc.scalar.copy, 2, 0, slice(0, 1))
-        for u, e in ((1, 0), (1, 1), (0, 1)):
-            lay_out(nc.vector.tensor_copy, 2, u, slice(e, e + 1))
-        for half in range(2):
-            quantize_w1(half)
+        middle_codes = placed.tile([P, SLICE], U32, name="middle_codes", align_bytes=ALIGN, offset=0)
+        late_codes = keep.tile([P, SLICE], U32, name="late_codes", align_bytes=ALIGN)
+        quantize_x(middle_codes[:, :GROUP], 2)
+        quantize_x(middle_codes[:, GROUP:], 3)
+        for g in range(4, groups):
+            staged.append(stage_x(nc.vector.tensor_copy, g, placed, offset=raw_offset + (g - 4) * STAGED_BYTES))
+        quantize_x(late_codes[:, :GROUP], 4)
+        w2_staged = keep.tile([P, N, PACK], BF16, name="w2_staged", align_bytes=ALIGN)
+        interleave(nc.vector.tensor_copy, w2_staged[:], w2_raw[:])
+        quantize_x(late_codes[:, GROUP:], 5)
 
-        def stage_x(copy, g, offset):
-            tile = reused.tile([P, GROUP, PACK], BF16, name=f"x_staged{g}", align_bytes=ALIGN, offset=offset)
-            start = g * GROUP - SLICE
-            interleave(copy, tile[:], late_rows[:, :, start : start + GROUP])
-            return tile
-
-        codes1 = reused.tile([P, GROUP], U32, name="codes1", align_bytes=ALIGN, offset=last_raw - 256)
-        quantize(nc, codes1[:], x_scales[:, GROUP:SLICE], x_first[:, GROUP:].rearrange("p n j -> p (n j)"))
-        ring = (last_raw + 256, last_raw + 256 + GROUP * PACK * 2)
-        staged = [stage_x(nc.vector.tensor_copy, 2, ring[0]), stage_x(nc.vector.tensor_copy, 3, ring[1])]
-        nc.scalar.activation(late_rows[:, 3, SLICE:], looked_up(3, 2 * SLICE, SLICE), COPY)
-        for k in range(2):
-            quantize_x(staged[k][:], (2 + k) * GROUP, GROUP)
-        w2_staged = reused.tile([P, N, PACK], BF16, name="w2_staged", align_bytes=ALIGN, offset=0)
-        nc.vector.tensor_copy(
-            w2_staged[:].rearrange("p (c i) t -> p c t i", i=4), w2_raw[:].rearrange("p t (c i) -> p c t i", i=4)
-        )
-        staged = [stage_x(nc.vector.tensor_copy, 4 + k, ring[k]) for k in range(2)]
-        quantize_x(staged[0][:], 4 * GROUP, GROUP)
-        w2_codes = keep.tile([P, N], U32, name="w2_codes", align_bytes=ALIGN)
-        w2_scales = keep.tile([P, N], U8, name="w2_scales", align_bytes=ALIGN)
-        quantize(nc, w2_codes[:], w2_scales[:], w2_staged[:].rearrange("p n t -> p (n t)"))
-        quantize_x(staged[1][:], 5 * GROUP, GROUP)
-
-        h_offset, h_bytes = 2048, SLICE * PACK * 2
+        h_offset, h_bytes = raw_offset + 2 * STAGED_BYTES, 2 * STAGED_BYTES
         h_staged = []
-        for s in range(slices):
-            tile = reused.tile(
+        for s in range(S // SLICE):
+            tile = placed.tile(
                 [P, SLICE, PACK], BF16, name=f"h_staged{s}", align_bytes=ALIGN, offset=h_offset + s * h_bytes
             )
             h_staged.append(tile)
-        h_banks = []
-        for g in range(groups):
-            bank = psum.tile([P, PACK, GROUP], F32, name=f"h_bank{g}")
-            h_banks.append(bank)
 
         def h_values(start, width):
             return h_staged[start // SLICE][:, start % SLICE : start % SLICE + width, :]
 
-        def gelu(start, width):
-            own = slice(start % GROUP, start % GROUP + width)
-            bank = h_banks[start // GROUP]
-            nc.scalar.activation(h_values(start, width), bank[:, :, own].rearrange("p t n -> p n t"), GELU)
-
         last = S - HALF
-        for g in range(groups):
-            start = g * GROUP
-            tokens = codes1[:] if g == 1 else x_codes[:, start : start + GROUP]
-            for u in SIDES:
-                for t in (2 * u, 2 * u + 1):
-                    cols = slice(t * P, (t + 1) * P)
-                    token_scales = x_scales[:, start : start + GROUP]
-                    multiply(nc, h_banks[g][:, t, :], w1_codes[:, cols], w1_scales[:, cols], tokens, token_scales)
-            if g < groups - 1:
-                gelu(start, GROUP)
-        gelu(last - HALF, HALF)
-        gelu(last, HALF)
+        for g in range(2, groups):
+            bank = psum.tile([P, PACK, GROUP], F32, name=f"h_bank{g}")
+            codes = (middle_codes, late_codes)[g // 4][:, g % 2 * GROUP : (g % 2 + 1) * GROUP]
+            for t in range(PACK):
+                multiply(nc, bank[:, t, :], *w1_tile(t), codes, x_scales[:, g * GROUP : (g + 1) * GROUP])
+            widths = (GROUP,) if g < groups - 1 else (HALF, HALF)
+            for piece, width in enumerate(widths):
+                own = bank[:, :, piece * HALF : piece * HALF + width].rearrange("p t n -> p n t")
+                nc.scalar.activation(h_values(g * GROUP + piece * HALF, width), own, GELU)
+
+        w2_codes = keep.tile([P, N], U32, name="w2_codes", align_bytes=ALIGN)
+        w2_scales = keep.tile([P, N], U8, name="w2_scales", align_bytes=ALIGN)
+        interleave(nc.vector.tensor_copy, h_staged[0][:], h_rows[:])
+        quantize(nc, w2_codes[:], w2_scales[:], flat(w2_staged[:]))
 
         h_codes = keep.tile([P, S], U32, name="h_codes", align_bytes=ALIGN)
         h_scales = keep.tile([P, S], U8, name="h_scales", align_bytes=ALIGN)
 
         def second_product(y, start, width):
             cols = slice(start, start + width)
-            quantize(nc, h_codes[:, cols], h_scales[:, cols], h_values(start, width).rearrange("p n t -> p (n t)"))
+            quantize(nc, h_codes[:, cols], h_scales[:, cols], flat(h_values(start, width)))
             multiply(nc, y, w2_codes[:], w2_scales[:], h_codes[:, cols], h_scales[:, cols])
 
         y_banks = []
         for s in range(2):
-            bank = psum.tile([P, SLICE], F32, name=f"y_bank{s}")
+            bank = psum.tile([P, SLICE], F32, name=f"y_bank{s}", tag=f"head_bank{s}")
             second_product(bank[:], s * SLICE, SLICE)
             y_banks.append(bank)
-        result0 = reused.tile([P, SLICE], F32, name="result0", align_bytes=ALIGN, offset=h_offset + h_bytes)
+        result0 = placed.tile([P, SLICE], F32, name="result0", align_bytes=ALIGN, offset=h_offset + h_bytes)
         nc.vector.tensor_copy(result0[:], y_banks[0][:])
-        nc.sync.dma_start(out=out[:, part(0)], in_=result0[:])
+        nc.sync.dma_start(out=out[:, :SLICE], in_=result0[:])
         result1 = keep.tile([P, SLICE], F32, name="result1")
         nc.scalar.copy(result1[:], y_banks[1][:])
-        nc.sync.dma_start(out=out[:, part(1)], in_=result1[:])
+        nc.sync.dma_start(out=out[:, SLICE : 2 * SLICE], in_=result1[:])
 
         result2 = keep.tile([P, SLICE], F32, name="result2")
-        y_late = psum.tile([P, SLICE - HALF], F32, name="y_late", tag="h_bank0")
-        y_last = psum.tile([P, HALF], F32, name="y_last", tag="h_bank1")
-        second_product(y_late[:, :GROUP], 2 * SLICE, GROUP)
-        second_product(y_late[:, GROUP:], last - HALF, HALF)
-        nc.scalar.copy(result2[:, : SLICE - HALF], y_late[:])
-        second_product(y_last[:], last, HALF)
-        nc.vector.tensor_copy(result2[:, SLICE - HALF :], y_last[:])
-        nc.sync.dma_start(out=out[:, part(2)], in_=result2[:])
+        pieces = ((0, GROUP, nc.scalar.copy), (GROUP, HALF, nc.scalar.copy), (GROUP + HALF, HALF, nc.vector.tensor_copy))
+        for piece, (start, width, copy) in enumerate(pieces):
+            bank = psum.tile([P, width], F32, name=f"y_late{piece}", tag=("head_bank2", "head_bank3", "h_bank2")[piece])
+            second_product(bank[:], 2 * SLICE + start, width)
+            copy(result2[:, start : start + width], bank[:])
+        nc.sync.dma_start(out=out[:, 2 * SLICE :], in_=result2[:])

@@ -22,6 +22,7 @@ HALF = 64
 ALIGN = 64
 NEIGHBOURS = 4
 WARM_M, WARM_N = 32, 512
+VECTOR_SHARE = 384
 STAGED_BYTES = GROUP * PACK * 2
 
 
@@ -83,24 +84,29 @@ def tile_picked_pick_mlp_gelu_sub_e_kernel(tc, xT, w1, w2, offs, out):
         nc.scalar.activation(table_out[:], table_in[:], GELU)
 
         picked = keep.tile([P, PACK, S], BF16, name="picked", align_bytes=ALIGN)
+        early = 2 * SLICE
+        early_staged = keep.tile([P, early, PACK], BF16, name="early_staged", align_bytes=ALIGN)
 
-        def gather(engine_copy, j, start, width):
+        def gather(copy, j, start, width):
             window = planes[j][:].indirect(offsets[:, start // 16 : (start + width) // 16])
-            engine_copy(picked[:, j, start : start + width], window)
+            copy(picked[:, j, start : start + width], window)
 
         def scalar_gather(to, window):
             nc.scalar.activation(to, window, COPY)
-
-        for j in range(PACK - 1):
-            gather(nc.vector.tensor_copy, j, 0, S // 2)
-            gather(scalar_gather, j, S // 2, S // 2)
 
         warm_codes = keep.tile([P, WARM_N + WARM_M], U32, name="warm_codes", align_bytes=ALIGN)
         warm_scales = keep.tile([P, WARM_N + HALF], U8, name="warm_scales", align_bytes=ALIGN)
         moving = slice(0, WARM_N)
         still = slice(WARM_N, WARM_N + WARM_M)
+
+        for j in range(PACK - 1):
+            gather(nc.vector.tensor_copy, j, 0, VECTOR_SHARE)
+            gather(scalar_gather, j, VECTOR_SHARE, S - VECTOR_SHARE)
         picked_rows = picked[:].rearrange("p j n -> p (j n)")
-        quantize(nc, warm_codes[:, moving], warm_scales[:, moving], picked_rows[:, : WARM_N * PACK])
+        for start in range(0, WARM_N, SLICE):
+            cols = slice(start, start + SLICE)
+            quantize(nc, warm_codes[:, cols], warm_scales[:, cols], picked_rows[:, : SLICE * PACK])
+        interleave(nc.vector.tensor_copy, early_staged[:, :, :2], picked[:, :2, :early])
 
         for g in range(2):
             gather(nc.vector.tensor_copy, 3, g * GROUP, GROUP)
@@ -113,22 +119,27 @@ def tile_picked_pick_mlp_gelu_sub_e_kernel(tc, xT, w1, w2, offs, out):
             stationary = (warm_codes[:, still], warm_scales[:, still])
             multiply(nc, warm_bank[:], *stationary, warm_codes[:, moving], warm_scales[:, moving])
 
-        def stage_x(copy, g, pool, **place):
-            tile = pool.tile([P, GROUP, PACK], BF16, name=f"x_staged{g}", align_bytes=ALIGN, **place)
-            interleave(copy, tile[:], picked[:, :, g * GROUP : (g + 1) * GROUP])
-            return tile
-
         x_scales = keep.tile([P, S], U8, name="x_scales", align_bytes=ALIGN)
-        head_codes = keep.tile([P, SLICE], U32, name="head_codes", align_bytes=ALIGN)
+        x_codes = keep.tile([P, S], U32, name="x_codes", align_bytes=ALIGN)
 
-        def quantize_x(codes, g):
-            quantize(nc, codes, x_scales[:, g * GROUP : (g + 1) * GROUP], flat(staged[g][:]))
+        def quantize_x(staged, start):
+            cols = slice(start, start + staged.shape[1])
+            quantize(nc, x_codes[:, cols], x_scales[:, cols], flat(staged))
 
-        staged = [stage_x(nc.vector.tensor_copy, g, keep) for g in range(2)]
-        quantize_x(head_codes[:, :GROUP], 0)
-        staged.append(stage_x(nc.vector.tensor_copy, 2, keep))
-        quantize_x(head_codes[:, GROUP:], 1)
-        staged.append(stage_x(nc.scalar.copy, 3, keep))
+        def group(g):
+            return slice(g * GROUP, (g + 1) * GROUP)
+
+        def finish_staging(copy, g):
+            interleave(copy, early_staged[:, group(g), 2:], picked[:, 2:, group(g)])
+
+        halves = (group(0), group(1))
+        finish_staging(nc.vector.tensor_copy, 0)
+        finish_staging(nc.vector.tensor_copy, 1)
+        quantize_x(early_staged[:, group(0)], 0)
+        finish_staging(nc.vector.tensor_copy, 2)
+        quantize_x(early_staged[:, group(1)], GROUP)
+        quantize_x(early_staged[:, group(2)], 2 * GROUP)
+        finish_staging(nc.scalar.copy, 3)
 
         w1_codes = keep.tile([P, H], U32, name="w1_codes", align_bytes=ALIGN)
         w1_scales = keep.tile([P, H], U8, name="w1_scales", align_bytes=ALIGN)
@@ -146,19 +157,16 @@ def tile_picked_pick_mlp_gelu_sub_e_kernel(tc, xT, w1, w2, offs, out):
         for t in range(PACK):
             quantize(nc, *w1_tile(t), flat(w1_staged[t][:]))
             bank = psum.tile([P, SLICE], F32, name=f"head_bank{t}")
-            multiply(nc, bank[:], *w1_tile(t), head_codes[:], x_scales[:, :SLICE])
+            multiply(nc, bank[:], *w1_tile(t), x_codes[:, :SLICE], x_scales[:, :SLICE])
             nc.scalar.activation(h_rows[:, t, :], bank[:], GELU)
 
-        middle_codes = placed.tile([P, SLICE], U32, name="middle_codes", align_bytes=ALIGN, offset=0)
-        late_codes = keep.tile([P, SLICE], U32, name="late_codes", align_bytes=ALIGN)
-        quantize_x(middle_codes[:, :GROUP], 2)
-        quantize_x(middle_codes[:, GROUP:], 3)
-        for g in range(4, groups):
-            staged.append(stage_x(nc.vector.tensor_copy, g, placed, offset=raw_offset + (g - 4) * STAGED_BYTES))
-        quantize_x(late_codes[:, :GROUP], 4)
-        w2_staged = keep.tile([P, N, PACK], BF16, name="w2_staged", align_bytes=ALIGN)
+        held_codes = placed.tile([P, GROUP], U32, name="held_codes", align_bytes=ALIGN, offset=3 * STAGED_BYTES)
+        quantize(nc, held_codes[:], x_scales[:, group(3)], flat(early_staged[:, group(3)]))
+        late_staged = placed.tile([P, SLICE, PACK], BF16, name="late_staged", align_bytes=ALIGN, offset=raw_offset)
+        interleave(nc.vector.tensor_copy, late_staged[:], picked[:, :, early:])
+        w2_staged = placed.tile([P, N, PACK], BF16, name="w2_staged", align_bytes=ALIGN, offset=STAGED_BYTES)
         interleave(nc.vector.tensor_copy, w2_staged[:], w2_raw[:])
-        quantize_x(late_codes[:, GROUP:], 5)
+        quantize_x(late_staged[:], 2 * SLICE)
 
         h_offset, h_bytes = raw_offset + 2 * STAGED_BYTES, 2 * STAGED_BYTES
         h_staged = []
@@ -174,7 +182,7 @@ def tile_picked_pick_mlp_gelu_sub_e_kernel(tc, xT, w1, w2, offs, out):
         last = S - HALF
         for g in range(2, groups):
             bank = psum.tile([P, PACK, GROUP], F32, name=f"h_bank{g}")
-            codes = (middle_codes, late_codes)[g // 4][:, g % 2 * GROUP : (g % 2 + 1) * GROUP]
+            codes = held_codes[:] if g == 3 else x_codes[:, group(g)]
             for t in range(PACK):
                 multiply(nc, bank[:, t, :], *w1_tile(t), codes, x_scales[:, g * GROUP : (g + 1) * GROUP])
             widths = (GROUP,) if g < groups - 1 else (HALF, HALF)
@@ -184,7 +192,8 @@ def tile_picked_pick_mlp_gelu_sub_e_kernel(tc, xT, w1, w2, offs, out):
 
         w2_codes = keep.tile([P, N], U32, name="w2_codes", align_bytes=ALIGN)
         w2_scales = keep.tile([P, N], U8, name="w2_scales", align_bytes=ALIGN)
-        interleave(nc.vector.tensor_copy, h_staged[0][:], h_rows[:])
+        for half in halves:
+            interleave(nc.vector.tensor_copy, h_staged[0][:, half], h_rows[:, :, half])
         quantize(nc, w2_codes[:], w2_scales[:], flat(w2_staged[:]))
 
         h_codes = keep.tile([P, S], U32, name="h_codes", align_bytes=ALIGN)
@@ -192,7 +201,10 @@ def tile_picked_pick_mlp_gelu_sub_e_kernel(tc, xT, w1, w2, offs, out):
 
         def second_product(y, start, width):
             cols = slice(start, start + width)
-            quantize(nc, h_codes[:, cols], h_scales[:, cols], flat(h_values(start, width)))
+            step = GROUP if start == 0 else width
+            for first in range(start, start + width, step):
+                own = slice(first, first + step)
+                quantize(nc, h_codes[:, own], h_scales[:, own], flat(h_values(first, step)))
             multiply(nc, y, w2_codes[:], w2_scales[:], h_codes[:, cols], h_scales[:, cols])
 
         y_banks = []

@@ -138,8 +138,7 @@ def tile_picked_pick_mlp_gelu_sub_e_kernel(tc, xT, w1, w2, offs, out):
         quantize_x(early_staged[:, group(0)], 0)
         finish_staging(nc.vector.tensor_copy, 2)
         quantize_x(early_staged[:, group(1)], GROUP)
-        quantize_x(early_staged[:, group(2)], 2 * GROUP)
-        finish_staging(nc.scalar.copy, 3)
+        finish_staging(nc.vector.tensor_copy, 3)
 
         w1_codes = keep.tile([P, H], U32, name="w1_codes", align_bytes=ALIGN)
         w1_scales = keep.tile([P, H], U8, name="w1_scales", align_bytes=ALIGN)
@@ -160,11 +159,11 @@ def tile_picked_pick_mlp_gelu_sub_e_kernel(tc, xT, w1, w2, offs, out):
             multiply(nc, bank[:], *w1_tile(t), x_codes[:, :SLICE], x_scales[:, :SLICE])
             nc.scalar.activation(h_rows[:, t, :], bank[:], GELU)
 
-        held_codes = placed.tile([P, GROUP], U32, name="held_codes", align_bytes=ALIGN, offset=3 * STAGED_BYTES)
-        quantize(nc, held_codes[:], x_scales[:, group(3)], flat(early_staged[:, group(3)]))
+        held_codes = placed.tile([P, SLICE], U32, name="held_codes", align_bytes=ALIGN, offset=0)
+        quantize(nc, held_codes[:], x_scales[:, SLICE:early], flat(early_staged[:, SLICE:]))
         late_staged = placed.tile([P, SLICE, PACK], BF16, name="late_staged", align_bytes=ALIGN, offset=raw_offset)
         interleave(nc.vector.tensor_copy, late_staged[:], picked[:, :, early:])
-        w2_staged = placed.tile([P, N, PACK], BF16, name="w2_staged", align_bytes=ALIGN, offset=STAGED_BYTES)
+        w2_staged = placed.tile([P, N, PACK], BF16, name="w2_staged", align_bytes=ALIGN, offset=3 * STAGED_BYTES)
         interleave(nc.vector.tensor_copy, w2_staged[:], w2_raw[:])
         quantize_x(late_staged[:], 2 * SLICE)
 
@@ -182,7 +181,7 @@ def tile_picked_pick_mlp_gelu_sub_e_kernel(tc, xT, w1, w2, offs, out):
         last = S - HALF
         for g in range(2, groups):
             bank = psum.tile([P, PACK, GROUP], F32, name=f"h_bank{g}")
-            codes = held_codes[:] if g == 3 else x_codes[:, group(g)]
+            codes = held_codes[:, group(g - 2)] if g < 4 else x_codes[:, group(g)]
             for t in range(PACK):
                 multiply(nc, bank[:, t, :], *w1_tile(t), codes, x_scales[:, g * GROUP : (g + 1) * GROUP])
             widths = (GROUP,) if g < groups - 1 else (HALF, HALF)

@@ -129,16 +129,16 @@ def tile_picked_pick_mlp_gelu_sub_e_kernel(tc, xT, w1, w2, offs, out):
         def group(g):
             return slice(g * GROUP, (g + 1) * GROUP)
 
-        def finish_staging(copy, g):
-            interleave(copy, early_staged[:, group(g), 2:], picked[:, 2:, group(g)])
+        def finish_staging(copy, tokens):
+            interleave(copy, early_staged[:, tokens, 2:], picked[:, 2:, tokens])
 
         halves = (group(0), group(1))
-        finish_staging(nc.vector.tensor_copy, 0)
-        finish_staging(nc.vector.tensor_copy, 1)
+        finish_staging(nc.vector.tensor_copy, group(0))
+        finish_staging(nc.vector.tensor_copy, group(1))
         quantize_x(early_staged[:, group(0)], 0)
-        finish_staging(nc.vector.tensor_copy, 2)
+        finish_staging(nc.vector.tensor_copy, slice(SLICE, SLICE + HALF))
         quantize_x(early_staged[:, group(1)], GROUP)
-        finish_staging(nc.vector.tensor_copy, 3)
+        finish_staging(nc.scalar.copy, slice(SLICE + HALF, early))
 
         w1_codes = keep.tile([P, H], U32, name="w1_codes", align_bytes=ALIGN)
         w1_scales = keep.tile([P, H], U8, name="w1_scales", align_bytes=ALIGN)

@@ -106,7 +106,8 @@ def tile_picked_pick_mlp_gelu_sub_e_kernel(tc, xT, w1, w2, offs, out):
         for start in range(0, WARM_N, SLICE):
             cols = slice(start, start + SLICE)
             quantize(nc, warm_codes[:, cols], warm_scales[:, cols], picked_rows[:, : SLICE * PACK])
-        interleave(nc.vector.tensor_copy, early_staged[:, :, :2], picked[:, :2, :early])
+        interleave(nc.vector.tensor_copy, early_staged[:, :SLICE, :2], picked[:, :2, :SLICE])
+        interleave(nc.scalar.copy, early_staged[:, SLICE:, :2], picked[:, :2, SLICE:early])
 
         for g in range(2):
             gather(nc.vector.tensor_copy, 3, g * GROUP, GROUP)

from contextlib import ExitStack

import concourse.mybir as mybir

K, T, S, H, N = 512, 2048, 768, 512, 128
FLOPS = 2 * S * H * (K + N)

F32 = mybir.dt.float32
BF16 = mybir.dt.bfloat16
U32 = mybir.dt.uint32
U16 = mybir.dt.uint16
U8 = mybir.dt.uint8
FP8X4 = mybir.dt.float8_e4m3fn_x4
GELU = mybir.ActivationFunctionType.Gelu_apprx_tanh
COPY = mybir.ActivationFunctionType.Copy

P = 128
PACK = 4
SLICE = 256
GROUP = 128
HALF = 64
ALIGN = 64
NEIGHBOURS = 4
WARM_M, WARM_N = 32, 512
VECTOR_SHARE = 384
STAGED_BYTES = GROUP * PACK * 2


def quantize(nc, codes, scales, values):
    nc.vector.quantize_mx(out=codes.bitcast(FP8X4), scales=scales, in_=values)


def multiply(nc, product, weights, weight_scales, tokens, token_scales):
    nc.tensor.matmul_mx(
        out=product,
        lhsT=weights.bitcast(FP8X4),
        lhsT_scale=weight_scales,
        rhs=tokens.bitcast(FP8X4),
        rhs_scale=token_scales,
        start=True,
        stop=True,
    )


def interleave(copy, staged, rows):
    copy(
        staged.rearrange("p (c i) j -> p c j i", i=NEIGHBOURS),
        rows.rearrange("p j (c i) -> p c j i", i=NEIGHBOURS),
    )


def flat(staged):
    return staged.rearrange("p n j -> p (n j)")


def tile_picked_pick_mlp_gelu_sub_e_kernel(tc, xT, w1, w2, offs, out):
    nc = tc.nc
    groups = S // GROUP

    with ExitStack() as ctx:
        keep = ctx.enter_context(tc.tile_pool(name="keep", bufs=1))
        placed = ctx.enter_context(tc.tile_pool(name="placed", bufs=1))
        psum = ctx.enter_context(tc.psum_pool(name="psum", bufs=1))

        offsets = keep.tile([P, S // 16], U16, name="offsets")
        x_rows = xT.rearrange("(p j) t -> p j t", j=PACK)
        planes = [keep.tile([P, T], F32, name=f"plane{j}") for j in range(PACK)]
        nc.sync.dma_start(out=planes[0][:], in_=x_rows[:, 0, :])
        nc.scalar.dma_start(out=planes[1][:], in_=x_rows[:, 1, :])
        nc.sync.dma_start(offsets[:], offs)
        for j in range(2, PACK):
            nc.sync.dma_start(out=planes[j][:], in_=x_rows[:, j, :])
        raw_offset = PACK * STAGED_BYTES
        w1_raw = placed.tile([P, PACK, H], F32, name="w1_raw", align_bytes=ALIGN, offset=raw_offset)
        nc.sync.dma_start(out=w1_raw[:], in_=w1.rearrange("(p j) h -> p j h", j=PACK))
        w2_raw = keep.tile([P, PACK, N], F32, name="w2_raw")
        w2_rows = w2.rearrange("(a t r) n -> r a t n", t=PACK, r=NEIGHBOURS)
        for r in range(NEIGHBOURS):
            nc.sync.dma_start(out=w2_raw[r::NEIGHBOURS], in_=w2_rows[r])

        table_in = keep.tile([P, 1], F32, name="table_in")
        nc.vector.memset(table_in[:], 0.0)
        table_out = keep.tile([P, 1], F32, name="table_out")
        nc.scalar.activation(table_out[:], table_in[:], GELU)

        picked = keep.tile([P, PACK, S], BF16, name="picked", align_bytes=ALIGN)
        early = 2 * SLICE
        early_staged = keep.tile([P, early, PACK], BF16, name="early_staged", align_bytes=ALIGN)

        def gather(copy, j, start, width):
            window = planes[j][:].indirect(offsets[:, start // 16 : (start + width) // 16])
            copy(picked[:, j, start : start + width], window)

        def scalar_gather(to, window):
            nc.scalar.activation(to, window, COPY)

        warm_codes = keep.tile([P, WARM_N + WARM_M], U32, name="warm_codes", align_bytes=ALIGN)
        warm_scales = keep.tile([P, WARM_N + HALF], U8, name="warm_scales", align_bytes=ALIGN)
        moving = slice(0, WARM_N)
        still = slice(WARM_N, WARM_N + WARM_M)

        for j in range(PACK - 1):
            gather(nc.vector.tensor_copy, j, 0, VECTOR_SHARE)
            gather(scalar_gather, j, VECTOR_SHARE, S - VECTOR_SHARE)
        picked_rows = picked[:].rearrange("p j n -> p (j n)")
        for start in range(0, WARM_N, SLICE):
            cols = slice(start, start + SLICE)
            quantize(nc, warm_codes[:, cols], warm_scales[:, cols], picked_rows[:, : SLICE * PACK])
        interleave(nc.vector.tensor_copy, early_staged[:, :SLICE, :2], picked[:, :2, :SLICE])
        interleave(nc.scalar.copy, early_staged[:, SLICE:, :2], picked[:, :2, SLICE:early])

        for g in range(2):
            gather(nc.vector.tensor_copy, 3, g * GROUP, GROUP)
        for s in range(1, 3):
            gather(scalar_gather, 3, s * SLICE, SLICE)

        quantize(nc, warm_codes[:, still], warm_scales[:, still], picked[:, 3, : WARM_M * PACK])
        warm_bank = psum.tile([WARM_M, WARM_N], F32, name="warm_bank", tag="h_bank5")
        for turn in range(3):
            stationary = (warm_codes[:, still], warm_scales[:, still])
            multiply(nc, warm_bank[:], *stationary, warm_codes[:, moving], warm_scales[:, moving])

        x_scales = keep.tile([P, S], U8, name="x_scales", align_bytes=ALIGN)
        x_codes = keep.tile([P, S], U32, name="x_codes", align_bytes=ALIGN)

        def quantize_x(staged, start):
            cols = slice(start, start + staged.shape[1])
            quantize(nc, x_codes[:, cols], x_scales[:, cols], flat(staged))

        def group(g):
            return slice(g * GROUP, (g + 1) * GROUP)

        def finish_staging(copy, tokens):
            interleave(copy, early_staged[:, tokens, 2:], picked[:, 2:, tokens])

        halves = (group(0), group(1))
        finish_staging(nc.vector.tensor_copy, group(0))
        finish_staging(nc.vector.tensor_copy, group(1))
        quantize_x(early_staged[:, group(0)], 0)
        finish_staging(nc.vector.tensor_copy, slice(SLICE, SLICE + HALF))
        quantize_x(early_staged[:, group(1)], GROUP)
        finish_staging(nc.scalar.copy, slice(SLICE + HALF, early))

        w1_codes = keep.tile([P, H], U32, name="w1_codes", align_bytes=ALIGN)
        w1_scales = keep.tile([P, H], U8, name="w1_scales", align_bytes=ALIGN)
        w1_tiles = w1_raw[:].rearrange("p j (a t r) -> p t a j r", t=PACK, r=NEIGHBOURS)
        w1_staged = []
        for t, copy in enumerate((nc.vector.tensor_copy, nc.scalar.copy, nc.vector.tensor_copy, nc.scalar.copy)):
            tile = placed.tile([P, P, PACK], BF16, name=f"w1_staged{t}", align_bytes=ALIGN, offset=t * STAGED_BYTES)
            copy(tile[:].rearrange("p (a r) j -> p a j r", r=NEIGHBOURS), w1_tiles[:, t])
            w1_staged.append(tile)

        def w1_tile(t):
            return w1_codes[:, t * P : (t + 1) * P], w1_scales[:, t * P : (t + 1) * P]

        h_rows = keep.tile([P, PACK, SLICE], BF16, name="h_rows", align_bytes=ALIGN)
        for t in range(PACK):
            quantize(nc, *w1_tile(t), flat(w1_staged[t][:]))
            bank = psum.tile([P, SLICE], F32, name=f"head_bank{t}")
            multiply(nc, bank[:], *w1_tile(t), x_codes[:, :SLICE], x_scales[:, :SLICE])
            nc.scalar.activation(h_rows[:, t, :], bank[:], GELU)

        held_codes = placed.tile([P, SLICE], U32, name="held_codes", align_bytes=ALIGN, offset=0)
        quantize(nc, held_codes[:], x_scales[:, SLICE:early], flat(early_staged[:, SLICE:]))
        late_staged = placed.tile([P, SLICE, PACK], BF16, name="late_staged", align_bytes=ALIGN, offset=raw_offset)
        interleave(nc.vector.tensor_copy, late_staged[:], picked[:, :, early:])
        w2_staged = placed.tile([P, N, PACK], BF16, name="w2_staged", align_bytes=ALIGN, offset=3 * STAGED_BYTES)
        interleave(nc.vector.tensor_copy, w2_staged[:], w2_raw[:])
        quantize_x(late_staged[:], 2 * SLICE)

        h_offset, h_bytes = raw_offset + 2 * STAGED_BYTES, 2 * STAGED_BYTES
        h_staged = []
        for s in range(S // SLICE):
            tile = placed.tile(
                [P, SLICE, PACK], BF16, name=f"h_staged{s}", align_bytes=ALIGN, offset=h_offset + s * h_bytes
            )
            h_staged.append(tile)

        def h_values(start, width):
            return h_staged[start // SLICE][:, start % SLICE : start % SLICE + width, :]

        last = S - HALF
        for g in range(2, groups):
            bank = psum.tile([P, PACK, GROUP], F32, name=f"h_bank{g}")
            codes = held_codes[:, group(g - 2)] if g < 4 else x_codes[:, group(g)]
            for t in range(PACK):
                multiply(nc, bank[:, t, :], *w1_tile(t), codes, x_scales[:, g * GROUP : (g + 1) * GROUP])
            widths = (GROUP,) if g < groups - 1 else (HALF, HALF)
            for piece, width in enumerate(widths):
                own = bank[:, :, piece * HALF : piece * HALF + width].rearrange("p t n -> p n t")
                nc.scalar.activation(h_values(g * GROUP + piece * HALF, width), own, GELU)

        w2_codes = keep.tile([P, N], U32, name="w2_codes", align_bytes=ALIGN)
        w2_scales = keep.tile([P, N], U8, name="w2_scales", align_bytes=ALIGN)
        for half in halves:
            interleave(nc.vector.tensor_copy, h_staged[0][:, half], h_rows[:, :, half])
        quantize(nc, w2_codes[:], w2_scales[:], flat(w2_staged[:]))

        h_codes = keep.tile([P, S], U32, name="h_codes", align_bytes=ALIGN)
        h_scales = keep.tile([P, S], U8, name="h_scales", align_bytes=ALIGN)

        def second_product(y, start, width):
            cols = slice(start, start + width)
            step = GROUP if start == 0 else width
            for first in range(start, start + width, step):
                own = slice(first, first + step)
                quantize(nc, h_codes[:, own], h_scales[:, own], flat(h_values(first, step)))
            multiply(nc, y, w2_codes[:], w2_scales[:], h_codes[:, cols], h_scales[:, cols])

        y_banks = []
        for s in range(2):
            bank = psum.tile([P, SLICE], F32, name=f"y_bank{s}", tag=f"head_bank{s}")
            second_product(bank[:], s * SLICE, SLICE)
            y_banks.append(bank)
        result0 = placed.tile([P, SLICE], F32, name="result0", align_bytes=ALIGN, offset=h_offset + h_bytes)
        nc.vector.tensor_copy(result0[:], y_banks[0][:])
        nc.sync.dma_start(out=out[:, :SLICE], in_=result0[:])
        result1 = keep.tile([P, SLICE], F32, name="result1")
        nc.scalar.copy(result1[:], y_banks[1][:])
        nc.sync.dma_start(out=out[:, SLICE : 2 * SLICE], in_=result1[:])

        result2 = keep.tile([P, SLICE], F32, name="result2")
        pieces = ((0, GROUP, nc.scalar.copy), (GROUP, HALF, nc.scalar.copy), (GROUP + HALF, HALF, nc.vector.tensor_copy))
        for piece, (start, width, copy) in enumerate(pieces):
            bank = psum.tile([P, width], F32, name=f"y_late{piece}", tag=("head_bank2", "head_bank3", "h_bank2")[piece])
            second_product(bank[:], 2 * SLICE + start, width)
            copy(result2[:, start : start + width], bank[:])
        nc.sync.dma_start(out=out[:, 2 * SLICE :], in_=result2[:])
